import numpy as np
import ml_dtypes


def mxq(x, axis, fmt="e4m3"):
    dtype, down = {"e4m3": (ml_dtypes.float8_e4m3fn, 7), "e5m2": (ml_dtypes.float8_e5m2, 14)}[fmt]
    v = np.moveaxis(np.asarray(x, np.float32).astype(ml_dtypes.bfloat16).astype(np.float64), axis, -1)
    blocks = v.reshape(v.shape[:-1] + (-1, 32))
    amax = np.abs(blocks).max(-1, keepdims=True)
    byte = np.maximum(np.where(amax > 0, np.frexp(amax)[1] - 1 + 127, 0) - down, 1)
    scale = np.exp2(byte - 127.0)
    codes = (blocks / scale).astype(np.float32).astype(dtype).astype(np.float64)
    return np.moveaxis((codes * scale).reshape(v.shape), -1, axis)


WIDE = False


def mx_kscale(k):
    if not WIDE:
        return np.ones(k)
    levels = np.array([10, -10, 5, -5, 0])
    if k % 512:
        return np.exp2(np.random.permutation(np.resize(levels, k // 32))).repeat(32)
    a = np.empty((k // 512, 16))
    for p in range(k // 512):
        a[p, :8] = np.random.permutation(np.resize(levels, 8))
        for g in range(8):
            far = levels[np.abs(levels - a[p, g]) >= 10]
            a[p, g + 8] = far[np.random.randint(len(far))]
    return np.exp2(a.ravel()).repeat(32)


def f64(x):
    return np.asarray(x).astype(np.float64)


def striped(idx):
    return np.tile(idx.reshape(-1, 16).T, (8, 1)).astype(np.uint16)


def unstriped(offs):
    return offs[:16].T.reshape(-1).astype(np.int64)


def pack_weight(w):
    k, n = w.shape
    w = f64(np.asarray(w, np.float32).astype(ml_dtypes.bfloat16)).reshape(k // 32, 32, n)
    amax = np.abs(w).max(1)
    byte = np.clip(np.where(amax > 0, np.frexp(amax)[1] - 1 + 127 - 7, 1), 1, 254)
    scaled = (w * np.exp2(127.0 - byte)[:, None, :]).reshape(k, n).astype(np.float32)
    words = np.ascontiguousarray(scaled.reshape(k // 512, 128, 4, n).transpose(0, 1, 3, 2)).astype(ml_dtypes.float8_e4m3fn).view(np.uint8)
    return words, np.ascontiguousarray(byte.astype(np.uint8).reshape(k // 512, 16, n))


def unpack_weight(words, scales):
    g, p, n, _ = words.shape
    vals = np.ascontiguousarray(words).view(ml_dtypes.float8_e4m3fn).astype(np.float64) * np.repeat(np.exp2(scales.astype(np.float64) - 127.0), 8, axis=1)[..., None]
    return vals.transpose(0, 1, 3, 2).reshape(g * 512, n)


E2M1 = np.array([0.0, 0.5, 1.0, 1.5, 2.0, 3.0, 4.0, 6.0, -0.0, -0.5, -1.0, -1.5, -2.0, -3.0, -4.0, -6.0])


def pack_fp4(w):
    k, n = w.shape
    w = f64(np.asarray(w, np.float32).astype(ml_dtypes.bfloat16)).reshape(k // 32, 32, n)
    amax = np.abs(w).max(1)
    mant, ex = np.frexp(amax / 6.0)
    byte = np.clip(np.where(amax > 0, np.where(mant > 0.5, ex, ex - 1) + 127, 1), 1, 254)
    scaled = (w * np.exp2(127.0 - byte)[:, None, :]).reshape(k, n).astype(np.float32)
    c = np.ascontiguousarray(scaled.reshape(k // 512, 128, 4, n).transpose(0, 1, 3, 2)).astype(ml_dtypes.float4_e2m1fn).view(np.uint8) & 0xF
    words = (c[..., 0::2] | (c[..., 1::2] << 4)).reshape(k // 512, 128, 2 * n)
    return np.ascontiguousarray(words), np.ascontiguousarray(byte.astype(np.uint8).reshape(k // 512, 16, n))


def unpack_fp4(words, scales):
    g, _, n = scales.shape
    words = np.ascontiguousarray(words).reshape(g, 128, n, 2)
    nib = np.empty((g, 128, n, 4), np.uint8)
    nib[..., 0::2] = words & 0xF
    nib[..., 1::2] = words >> 4
    vals = E2M1[nib] * np.repeat(np.exp2(scales.astype(np.float64) - 127.0), 8, axis=1)[..., None]
    return vals.transpose(0, 1, 3, 2).reshape(g * 512, n)


def planes(y):
    n, m = y.shape
    v = y.astype(np.float32).astype(ml_dtypes.bfloat16).astype(np.float64).reshape(n // 32, 32, m)
    top = np.abs(v).max(1)
    byte = np.clip(np.where(top > 0, np.frexp(top)[1] - 1 + 127 - 7, 1), 1, 254)
    codes = (v * np.exp2(127.0 - byte)[:, None, :]).reshape(n, m).astype(np.float32).astype(ml_dtypes.float8_e4m3fn).view(np.uint8)
    words = codes.reshape(n // 512, 128, 4, m).transpose(0, 1, 3, 2)
    return np.ascontiguousarray(words), np.ascontiguousarray(byte.astype(np.uint8).reshape(n // 512, 16, m))


K, T, S, H = 512, 2048, 1024, 512


def setup_inputs():
    n = np.random.standard_normal
    s = mx_kscale(K)[:, None]
    u = mx_kscale(H)
    packed_xT = pack_weight(n((K, T)) * s)
    packed_w2 = pack_fp4(n((H, H)) / np.sqrt(H) / u[:, None])
    return {
        "x_words": packed_xT[0],
        "x_scales": packed_xT[1],
        "w1": (n((K, H)) / np.sqrt(K) / s * u).astype(np.float32),
        "w2_words": packed_w2[0],
        "w2_scales": packed_w2[1],
        "pos": (0.5 * n((H, S)) * u[:, None]).astype(np.float32),
        "offs": striped(np.random.permutation(T)[(T * np.random.uniform(0, 1, S) ** 4).astype(np.int64)]),
    }


def reference(x_words, x_scales, w1, w2_words, w2_scales, pos, offs):
    xq = unpack_weight(x_words, x_scales)[:, unstriped(offs)]
    h = (mxq(f64(w1), 0, "e4m3").T @ xq) + f64(pos)
    out_0 = unpack_fp4(w2_words, w2_scales).T @ mxq(h, 0, "e4m3")
    return (out_0,) + planes(out_0)

@@ -1,0 +1,207 @@
+from contextlib import ExitStack
+
+import concourse.mybir as mybir
+
+K, T, S, H = 512, 2048, 1024, 512
+FLOPS = 2 * K * H * S + 2 * H * H * S
+
+F32 = mybir.dt.float32
+BF16 = mybir.dt.bfloat16
+I32 = mybir.dt.int32
+U32 = mybir.dt.uint32
+U16 = mybir.dt.uint16
+U8 = mybir.dt.uint8
+FP8X4 = mybir.dt.float8_e4m3fn_x4
+FP4X4 = mybir.dt.float4_e2m1fn_x4
+
+P = 128
+PACK = 4
+BLK = 128
+NBLK = S // BLK
+GATH = 256
+POS_CHUNKS = ((0, 256), (256, 512), (512, 1024))
+VEC_ROUND = (2, 4)
+OUT_CHUNKS = ((0, 256), (256, 512), (512, 768), (768, 896), (896, 1024))
+
+
+def tile_picked_embpos_none_po_kernel(
+    tc, x_words, x_scales, w1, w2_words, w2_scales, pos, offs, out_0, out_1, out_2
+):
+    nc = tc.nc
+    add = mybir.AluOpType.add
+    with ExitStack() as ctx:
+        keep = ctx.enter_context(tc.tile_pool(name="keep", bufs=1))
+        ring = ctx.enter_context(tc.tile_pool(name="ring", bufs=3))
+        ps_h = ctx.enter_context(tc.psum_pool(name="ps_h", bufs=4))
+        ps_y = ctx.enter_context(tc.psum_pool(name="ps_y", bufs=4))
+
+        offsets = keep.tile([P, S // 16], U16, name="offsets")
+        xw = keep.tile([P, T], I32, name="xw", align_bytes=64)
+        xs = keep.tile([P, T], U8, name="xs", align_bytes=64)
+        w2s_raw = keep.tile([P, H], U8, name="w2s_raw", align_bytes=64)
+        w2w_raw = keep.tile([P, 2 * H], U8, name="w2w_raw", align_bytes=64)
+        w1_raw = [keep.tile([P, PACK, H // 2], F32, name=f"w1_raw{a}", align_bytes=64) for a in range(2)]
+        pos_sb = [
+            keep.tile([P, PACK, b - a], F32, name=f"pos{a}", tag=f"slot{a}", align_bytes=64)
+            for a, b in POS_CHUNKS
+        ]
+
+        nc.vector.memset(xs[:].bitcast(I32), 0)
+        nc.vector.memset(w2s_raw[:].bitcast(I32), 0)
+
+        w1_rows = w1.rearrange("(p j) c -> p j c", j=PACK)
+        pos_rows = pos.rearrange("(p t) n -> p t n", t=PACK)
+        nc.sync.dma_start(offsets[:], offs)
+        nc.sync.dma_start(w2w_raw[:].bitcast(I32), w2_words[0].bitcast(I32))
+        nc.sync.dma_start(w1_raw[0][:], w1_rows[:, :, 0 : H // 2])
+        for q in range(4):
+            nc.sync.dma_start(
+                xs[32 * q : 32 * q + 4, :].bitcast(I32), x_scales[0, 4 * q : 4 * q + 4, :].bitcast(I32)
+            )
+        nc.sync.dma_start(w1_raw[1][:], w1_rows[:, :, H // 2 : H])
+        nc.sync.dma_start(xw[:], x_words[0].rearrange("p n t -> p (n t)").bitcast(I32))
+        for q in range(4):
+            nc.sync.dma_start(
+                w2s_raw[32 * q : 32 * q + 4, :].bitcast(I32),
+                w2_scales[0, 4 * q : 4 * q + 4, :].bitcast(I32),
+            )
+        for c, (a, b) in enumerate(POS_CHUNKS):
+            nc.sync.dma_start(pos_sb[c][:], pos_rows[:, :, a:b])
+
+        w2w = keep.tile([P, 2 * H], U8, name="w2w", align_bytes=64)
+        w2s = keep.tile([P, H], U8, name="w2s", align_bytes=64)
+        nc.vector.tensor_copy(
+            w2w[:].rearrange("p (t m e) -> p t m e", t=PACK, e=2),
+            w2w_raw[:].rearrange("p (m t e) -> p t m e", t=PACK, e=2),
+        )
+
+        gs = [keep.tile([P, 512], U8, name=f"gs{c}", align_bytes=64) for c in range(2)]
+        gw = {}
+        nc.vector.tensor_copy(gs[0][:], xs[:].indirect(offsets[:, 0:32]))
+        nc.vector.tensor_copy(gs[1][:], xs[:].indirect(offsets[:, 32:64]))
+
+        w1b = keep.tile([P, PACK * H], BF16, name="w1b", align_bytes=64)
+        w1c = keep.tile([P, H], U32, name="w1c", align_bytes=64)
+        w1s = keep.tile([P, H], U8, name="w1s", align_bytes=64)
+        w1b_v = w1b[:].rearrange("p (t m j) -> p m j t", t=PACK, j=PACK)
+        for a in range(2):
+            nc.scalar.copy(
+                w1b_v[:, 64 * a : 64 * (a + 1)], w1_raw[a][:].rearrange("p j (m t) -> p m j t", t=PACK)
+            )
+        nc.vector.quantize_mx(out=w1c[:].bitcast(FP8X4), scales=w1s[:], in_=w1b[:])
+
+        def gather_words(c):
+            tag = f"gw{c}" if c < 2 else f"slot{POS_CHUNKS[c - 2][0]}"
+            gw[c] = keep.tile([P, GATH], U32, name=f"gw{c}", tag=tag, align_bytes=64)
+            nc.vector.tensor_copy(
+                gw[c][:], xw[:].bitcast(U32).indirect(offsets[:, 16 * c : 16 * (c + 1)])
+            )
+
+        gather_words(0)
+        gather_words(1)
+        nc.vector.tensor_copy(
+            w2s[:].rearrange("p (t m) -> p t m", t=PACK),
+            w2s_raw[:].rearrange("p (m t) -> p t m", t=PACK),
+        )
+
+        y_sb = [keep.tile([P, PACK, b - a], F32, name=f"y{a}", align_bytes=64) for a, b in OUT_CHUNKS]
+        yb = [keep.tile([P, PACK * (b - a)], BF16, name=f"yb{a}", align_bytes=64) for a, b in OUT_CHUNKS]
+        yc = [keep.tile([P, b - a], I32, name=f"yc{a}", align_bytes=64) for a, b in OUT_CHUNKS]
+        ys = keep.tile([P, S], U8, name="ys", align_bytes=64)
+        out_rows = out_0.rearrange("(p t) n -> p t n", t=PACK)
+        out_words = out_1[0].rearrange("p n t -> p (n t)").bitcast(I32)
+
+        acc_h, hb, hq, acc_y = {}, {}, {}, {}
+
+        def first_product(b):
+            acc = ps_h.tile([P, PACK, BLK], F32, name="acc_h")
+            g, o = divmod(b * BLK, GATH)
+            g2, o2 = divmod(b * BLK, 512)
+            for t in range(PACK):
+                nc.tensor.matmul_mx(
+                    out=acc[:, t, :],
+                    lhsT=w1c[:, t * P : (t + 1) * P].bitcast(FP8X4),
+                    lhsT_scale=w1s[:, t * P : (t + 1) * P],
+                    rhs=gw[g][:, o : o + BLK].bitcast(FP8X4),
+                    rhs_scale=gs[g2][:, o2 : o2 + BLK],
+                    start=True,
+                    stop=True,
+                )
+            return acc
+
+        def add_pos(b, acc):
+            c = [n for n, (lo, hi) in enumerate(POS_CHUNKS) if lo <= b * BLK < hi][0]
+            o = b * BLK - POS_CHUNKS[c][0]
+            h16 = ring.tile([P, PACK * BLK], BF16, name="h16", align_bytes=64)
+            nc.vector.tensor_tensor(
+                h16[:].rearrange("p (c i t) -> p c t i", i=4, t=PACK),
+                acc[:].rearrange("p t (c i) -> p c t i", i=4),
+                pos_sb[c][:, :, o : o + BLK].rearrange("p t (c i) -> p c t i", i=4),
+                add,
+            )
+            return h16
+
+        def quant_h(h16):
+            hc = ring.tile([P, BLK], U32, name="hc", align_bytes=64)
+            hs = ring.tile([P, BLK], U8, name="hs", align_bytes=64)
+            nc.vector.quantize_mx(out=hc[:].bitcast(FP8X4), scales=hs[:], in_=h16[:])
+            return hc, hs
+
+        def second_product(hc, hs):
+            acc = ps_y.tile([P, PACK, BLK], F32, name="acc_y")
+            for t in range(PACK):
+                nc.tensor.matmul_mx(
+                    out=acc[:, t, :],
+                    lhsT=w2w[:, 2 * t * P : 2 * (t + 1) * P].bitcast(FP4X4),
+                    lhsT_scale=w2s[:, t * P : (t + 1) * P],
+                    rhs=hc[:].bitcast(FP8X4),
+                    rhs_scale=hs[:],
+                    start=True,
+                    stop=True,
+                )
+            return acc
+
+        def leave(b, acc):
+            c = [n for n, (lo, hi) in enumerate(OUT_CHUNKS) if lo <= b * BLK < hi][0]
+            lo, hi = OUT_CHUNKS[c]
+            o = b * BLK - lo
+            dst = yb[c][:, PACK * o : PACK * (o + BLK)]
+            if b not in VEC_ROUND:
+                nc.scalar.copy(
+                    dst.rearrange("p (n t) -> p n t", t=PACK), acc[:].rearrange("p t n -> p n t")
+                )
+            nc.scalar.copy(y_sb[c][:, :, o : o + BLK], acc[:])
+            if b in VEC_ROUND:
+                nc.vector.tensor_copy(
+                    dst.rearrange("p (c i t) -> p c t i", i=4, t=PACK),
+                    y_sb[c][:, :, o : o + BLK].rearrange("p t (c i) -> p c t i", i=4),
+                )
+            if (b + 1) * BLK == hi:
+                nc.sync.dma_start(out_rows[:, :, lo:hi], y_sb[c][:])
+
+        def quant_y(c):
+            lo, hi = OUT_CHUNKS[c]
+            nc.vector.quantize_mx(out=yc[c][:].bitcast(FP8X4), scales=ys[:, lo:hi], in_=yb[c][:])
+            nc.sync.dma_start(out_words[:, lo:hi], yc[c][:])
+
+        ends = {hi // BLK - 1: c for c, (lo, hi) in enumerate(OUT_CHUNKS)}
+        for s in range(NBLK + 4):
+            if s < NBLK:
+                acc_h[s] = first_product(s)
+            if 0 <= s - 1 < NBLK:
+                hb[s - 1] = add_pos(s - 1, acc_h[s - 1])
+            if 0 <= s - 2 < NBLK:
+                hq[s - 2] = quant_h(hb[s - 2])
+                acc_y[s - 2] = second_product(*hq[s - 2])
+            if s in (2, 4):
+                gather_words(s // 2 + 1)
+            if 0 <= s - 3 < NBLK:
+                leave(s - 3, acc_y[s - 3])
+            if s - 4 in ends:
+                quant_y(ends[s - 4])
+
+        for q in range(4):
+            eng = nc.sync if q % 2 == 0 else nc.scalar
+            eng.dma_start(
+                out_2[0, 4 * q : 4 * q + 4, :].bitcast(I32), ys[32 * q : 32 * q + 4, :].bitcast(I32)
+            )

@@ -20,7 +20,8 @@ BLK = 128
 NBLK = S // BLK
 GATH = 256
 POS_CHUNKS = ((0, 256), (256, 512), (512, 1024))
-VEC_ROUND = (2, 4)
+EARLY = 768
+VEC_ROUND = (3,)
 OUT_CHUNKS = ((0, 256), (256, 512), (512, 768), (768, 896), (896, 1024))
 
 
@@ -55,16 +56,11 @@ def tile_picked_embpos_none_po_kernel(
         nc.sync.dma_start(w2w_raw[:].bitcast(I32), w2_words[0].bitcast(I32))
         nc.sync.dma_start(w1_raw[0][:], w1_rows[:, :, 0 : H // 2])
         for q in range(4):
-            nc.sync.dma_start(
-                xs[32 * q : 32 * q + 4, :].bitcast(I32), x_scales[0, 4 * q : 4 * q + 4, :].bitcast(I32)
-            )
+            nc.sync.dma_start(xs[q:P:32, :].bitcast(I32), x_scales[0, q:16:4, :].bitcast(I32))
         nc.sync.dma_start(w1_raw[1][:], w1_rows[:, :, H // 2 : H])
         nc.sync.dma_start(xw[:], x_words[0].rearrange("p n t -> p (n t)").bitcast(I32))
         for q in range(4):
-            nc.sync.dma_start(
-                w2s_raw[32 * q : 32 * q + 4, :].bitcast(I32),
-                w2_scales[0, 4 * q : 4 * q + 4, :].bitcast(I32),
-            )
+            nc.sync.dma_start(w2s_raw[q:P:32, :].bitcast(I32), w2_scales[0, q:16:4, :].bitcast(I32))
         for c, (a, b) in enumerate(POS_CHUNKS):
             nc.sync.dma_start(pos_sb[c][:], pos_rows[:, :, a:b])
 
@@ -177,21 +173,30 @@ def tile_picked_embpos_none_po_kernel(
                     y_sb[c][:, :, o : o + BLK].rearrange("p t (c i) -> p c t i", i=4),
                 )
             if (b + 1) * BLK == hi:
-                nc.sync.dma_start(out_rows[:, :, lo:hi], y_sb[c][:])
+                eng = nc.scalar if hi == S else nc.sync
+                eng.dma_start(out_rows[:, :, lo:hi], y_sb[c][:])
 
         def quant_y(c):
             lo, hi = OUT_CHUNKS[c]
             nc.vector.quantize_mx(out=yc[c][:].bitcast(FP8X4), scales=ys[:, lo:hi], in_=yb[c][:])
             nc.sync.dma_start(out_words[:, lo:hi], yc[c][:])
+            if hi == EARLY:
+                for q in range(4):
+                    nc.sync.dma_start(
+                        out_2[0, q:16:4, 0:EARLY].bitcast(I32), ys[q:P:32, 0:EARLY].bitcast(I32)
+                    )
 
         ends = {hi // BLK - 1: c for c, (lo, hi) in enumerate(OUT_CHUNKS)}
         for s in range(NBLK + 4):
             if s < NBLK:
                 acc_h[s] = first_product(s)
+            if s == 2:
+                hq[0] = quant_h(hb[0])
             if 0 <= s - 1 < NBLK:
                 hb[s - 1] = add_pos(s - 1, acc_h[s - 1])
             if 0 <= s - 2 < NBLK:
-                hq[s - 2] = quant_h(hb[s - 2])
+                if s > 2:
+                    hq[s - 2] = quant_h(hb[s - 2])
                 acc_y[s - 2] = second_product(*hq[s - 2])
             if s in (2, 4):
                 gather_words(s // 2 + 1)
@@ -203,5 +208,5 @@ def tile_picked_embpos_none_po_kernel(
         for q in range(4):
             eng = nc.sync if q % 2 == 0 else nc.scalar
             eng.dma_start(
-                out_2[0, 4 * q : 4 * q + 4, :].bitcast(I32), ys[32 * q : 32 * q + 4, :].bitcast(I32)
+                out_2[0, q:16:4, EARLY:S].bitcast(I32), ys[q:P:32, EARLY:S].bitcast(I32)
             )

@@ -20,7 +20,8 @@ BLK = 128
 NBLK = S // BLK
 GATH = 256
 POS_CHUNKS = ((0, 256), (256, 512), (512, 1024))
-EARLY = 768
+Y_CHUNKS = ((0, 256), (256, 512), (512, 640), (640, 768), (768, 896), (896, 1024))
+WORD_CHUNKS = ((0, 512), (512, 896), (896, 1024))
 VEC_ROUND = (3,)
 OUT_CHUNKS = ((0, 256), (256, 512), (512, 768), (768, 896), (896, 1024))
 
@@ -79,10 +80,10 @@ def tile_picked_embpos_none_po_kernel(
         w1b = keep.tile([P, PACK * H], BF16, name="w1b", align_bytes=64)
         w1c = keep.tile([P, H], U32, name="w1c", align_bytes=64)
         w1s = keep.tile([P, H], U8, name="w1s", align_bytes=64)
-        w1b_v = w1b[:].rearrange("p (t m j) -> p m j t", t=PACK, j=PACK)
+        w1b_v = w1b[:].rearrange("p (t m j) -> p m t j", t=PACK, j=PACK)
         for a in range(2):
             nc.scalar.copy(
-                w1b_v[:, 64 * a : 64 * (a + 1)], w1_raw[a][:].rearrange("p j (m t) -> p m j t", t=PACK)
+                w1b_v[:, 64 * a : 64 * (a + 1)], w1_raw[a][:].rearrange("p j (m t) -> p m t j", t=PACK)
             )
         nc.vector.quantize_mx(out=w1c[:].bitcast(FP8X4), scales=w1s[:], in_=w1b[:])
 
@@ -100,9 +101,9 @@ def tile_picked_embpos_none_po_kernel(
             w2s_raw[:].rearrange("p (m t) -> p t m", t=PACK),
         )
 
-        y_sb = [keep.tile([P, PACK, b - a], F32, name=f"y{a}", align_bytes=64) for a, b in OUT_CHUNKS]
+        y_sb = [keep.tile([P, PACK, b - a], F32, name=f"y{a}", align_bytes=64) for a, b in Y_CHUNKS]
         yb = [keep.tile([P, PACK * (b - a)], BF16, name=f"yb{a}", align_bytes=64) for a, b in OUT_CHUNKS]
-        yc = [keep.tile([P, b - a], I32, name=f"yc{a}", align_bytes=64) for a, b in OUT_CHUNKS]
+        yc = keep.tile([P, S], I32, name="yc", align_bytes=64)
         ys = keep.tile([P, S], U8, name="ys", align_bytes=64)
         out_rows = out_0.rearrange("(p t) n -> p t n", t=PACK)
         out_words = out_1[0].rearrange("p n t -> p (n t)").bitcast(I32)
@@ -159,32 +160,30 @@ def tile_picked_embpos_none_po_kernel(
 
         def leave(b, acc):
             c = [n for n, (lo, hi) in enumerate(OUT_CHUNKS) if lo <= b * BLK < hi][0]
-            lo, hi = OUT_CHUNKS[c]
-            o = b * BLK - lo
+            o = b * BLK - OUT_CHUNKS[c][0]
             dst = yb[c][:, PACK * o : PACK * (o + BLK)]
+            d = [n for n, (lo, hi) in enumerate(Y_CHUNKS) if lo <= b * BLK < hi][0]
+            lo, hi = Y_CHUNKS[d]
+            y_blk = y_sb[d][:, :, b * BLK - lo : (b + 1) * BLK - lo]
             if b not in VEC_ROUND:
                 nc.scalar.copy(
                     dst.rearrange("p (n t) -> p n t", t=PACK), acc[:].rearrange("p t n -> p n t")
                 )
-            nc.scalar.copy(y_sb[c][:, :, o : o + BLK], acc[:])
+            nc.scalar.copy(y_blk, acc[:])
             if b in VEC_ROUND:
                 nc.vector.tensor_copy(
                     dst.rearrange("p (c i t) -> p c t i", i=4, t=PACK),
-                    y_sb[c][:, :, o : o + BLK].rearrange("p t (c i) -> p c t i", i=4),
+                    y_blk.rearrange("p t (c i) -> p c t i", i=4),
                 )
             if (b + 1) * BLK == hi:
-                eng = nc.scalar if hi == S else nc.sync
-                eng.dma_start(out_rows[:, :, lo:hi], y_sb[c][:])
+                nc.sync.dma_start(out_rows[:, :, lo:hi], y_sb[d][:])
 
         def quant_y(c):
             lo, hi = OUT_CHUNKS[c]
-            nc.vector.quantize_mx(out=yc[c][:].bitcast(FP8X4), scales=ys[:, lo:hi], in_=yb[c][:])
-            nc.sync.dma_start(out_words[:, lo:hi], yc[c][:])
-            if hi == EARLY:
-                for q in range(4):
-                    nc.sync.dma_start(
-                        out_2[0, q:16:4, 0:EARLY].bitcast(I32), ys[q:P:32, 0:EARLY].bitcast(I32)
-                    )
+            nc.vector.quantize_mx(out=yc[:, lo:hi].bitcast(FP8X4), scales=ys[:, lo:hi], in_=yb[c][:])
+            for a, b in WORD_CHUNKS:
+                if b == hi:
+                    nc.sync.dma_start(out_words[:, a:b], yc[:, a:b])
 
         ends = {hi // BLK - 1: c for c, (lo, hi) in enumerate(OUT_CHUNKS)}
         for s in range(NBLK + 4):
@@ -207,6 +206,4 @@ def tile_picked_embpos_none_po_kernel(
 
         for q in range(4):
             eng = nc.sync if q % 2 == 0 else nc.scalar
-            eng.dma_start(
-                out_2[0, q:16:4, EARLY:S].bitcast(I32), ys[q:P:32, EARLY:S].bitcast(I32)
-            )
+            eng.dma_start(out_2[0, q:16:4, :].bitcast(I32), ys[q:P:32, :].bitcast(I32))

@@ -23,6 +23,8 @@ POS_CHUNKS = ((0, 256), (256, 512), (512, 1024))
 Y_CHUNKS = ((0, 256), (256, 512), (512, 640), (640, 768), (768, 896), (896, 1024))
 WORD_CHUNKS = ((0, 512), (512, 896), (896, 1024))
 VEC_ROUND = (3,)
+VEC_PSUM = (7,)
+RUN = 2
 OUT_CHUNKS = ((0, 256), (256, 512), (512, 768), (768, 896), (896, 1024))
 
 
@@ -53,11 +55,12 @@ def tile_picked_embpos_none_po_kernel(
 
         w1_rows = w1.rearrange("(p j) c -> p j c", j=PACK)
         pos_rows = pos.rearrange("(p t) n -> p t n", t=PACK)
-        nc.sync.dma_start(offsets[:], offs)
         nc.sync.dma_start(w2w_raw[:].bitcast(I32), w2_words[0].bitcast(I32))
         nc.sync.dma_start(w1_raw[0][:], w1_rows[:, :, 0 : H // 2])
+        nc.sync.dma_start(offsets[:], offs)
         for q in range(4):
-            nc.sync.dma_start(xs[q:P:32, :].bitcast(I32), x_scales[0, q:16:4, :].bitcast(I32))
+            eng = nc.sync if q % 2 == 0 else nc.scalar
+            eng.dma_start(xs[q:P:32, :].bitcast(I32), x_scales[0, q:16:4, :].bitcast(I32))
         nc.sync.dma_start(w1_raw[1][:], w1_rows[:, :, H // 2 : H])
         nc.sync.dma_start(xw[:], x_words[0].rearrange("p n t -> p (n t)").bitcast(I32))
         for q in range(4):
@@ -131,9 +134,9 @@ def tile_picked_embpos_none_po_kernel(
             o = b * BLK - POS_CHUNKS[c][0]
             h16 = ring.tile([P, PACK * BLK], BF16, name="h16", align_bytes=64)
             nc.vector.tensor_tensor(
-                h16[:].rearrange("p (c i t) -> p c t i", i=4, t=PACK),
-                acc[:].rearrange("p t (c i) -> p c t i", i=4),
-                pos_sb[c][:, :, o : o + BLK].rearrange("p t (c i) -> p c t i", i=4),
+                h16[:].rearrange("p (c i t) -> p c t i", i=RUN, t=PACK),
+                acc[:].rearrange("p t (c i) -> p c t i", i=RUN),
+                pos_sb[c][:, :, o : o + BLK].rearrange("p t (c i) -> p c t i", i=RUN),
                 add,
             )
             return h16
@@ -165,15 +168,19 @@ def tile_picked_embpos_none_po_kernel(
             d = [n for n, (lo, hi) in enumerate(Y_CHUNKS) if lo <= b * BLK < hi][0]
             lo, hi = Y_CHUNKS[d]
             y_blk = y_sb[d][:, :, b * BLK - lo : (b + 1) * BLK - lo]
-            if b not in VEC_ROUND:
+            if b in VEC_PSUM:
+                nc.vector.tensor_copy(
+                    dst.rearrange("p (n t) -> p n t", t=PACK), acc[:].rearrange("p t n -> p n t")
+                )
+            elif b not in VEC_ROUND:
                 nc.scalar.copy(
                     dst.rearrange("p (n t) -> p n t", t=PACK), acc[:].rearrange("p t n -> p n t")
                 )
             nc.scalar.copy(y_blk, acc[:])
             if b in VEC_ROUND:
                 nc.vector.tensor_copy(
-                    dst.rearrange("p (c i t) -> p c t i", i=4, t=PACK),
-                    y_blk.rearrange("p t (c i) -> p c t i", i=4),
+                    dst.rearrange("p (c i t) -> p c t i", i=RUN, t=PACK),
+                    y_blk.rearrange("p t (c i) -> p c t i", i=RUN),
                 )
             if (b + 1) * BLK == hi:
                 nc.sync.dma_start(out_rows[:, :, lo:hi], y_sb[d][:])

@@ -25,6 +25,7 @@ WORD_CHUNKS = ((0, 512), (512, 896), (896, 1024))
 VEC_ROUND = (3,)
 VEC_PSUM = (7,)
 RUN = 2
+CAST_SPLIT = 48
 OUT_CHUNKS = ((0, 256), (256, 512), (512, 768), (768, 896), (896, 1024))
 
 
@@ -44,7 +45,7 @@ def tile_picked_embpos_none_po_kernel(
         xs = keep.tile([P, T], U8, name="xs", align_bytes=64)
         w2s_raw = keep.tile([P, H], U8, name="w2s_raw", align_bytes=64)
         w2w_raw = keep.tile([P, 2 * H], U8, name="w2w_raw", align_bytes=64)
-        w1_raw = [keep.tile([P, PACK, H // 2], F32, name=f"w1_raw{a}", align_bytes=64) for a in range(2)]
+        w1_raw = keep.tile([P, PACK, H], F32, name="w1_raw", align_bytes=64)
         pos_sb = [
             keep.tile([P, PACK, b - a], F32, name=f"pos{a}", tag=f"slot{a}", align_bytes=64)
             for a, b in POS_CHUNKS
@@ -56,12 +57,11 @@ def tile_picked_embpos_none_po_kernel(
         w1_rows = w1.rearrange("(p j) c -> p j c", j=PACK)
         pos_rows = pos.rearrange("(p t) n -> p t n", t=PACK)
         nc.sync.dma_start(w2w_raw[:].bitcast(I32), w2_words[0].bitcast(I32))
-        nc.sync.dma_start(w1_raw[0][:], w1_rows[:, :, 0 : H // 2])
         nc.sync.dma_start(offsets[:], offs)
         for q in range(4):
             eng = nc.sync if q % 2 == 0 else nc.scalar
             eng.dma_start(xs[q:P:32, :].bitcast(I32), x_scales[0, q:16:4, :].bitcast(I32))
-        nc.sync.dma_start(w1_raw[1][:], w1_rows[:, :, H // 2 : H])
+        nc.sync.dma_start(w1_raw[:], w1_rows)
         nc.sync.dma_start(xw[:], x_words[0].rearrange("p n t -> p (n t)").bitcast(I32))
         for q in range(4):
             nc.sync.dma_start(w2s_raw[q:P:32, :].bitcast(I32), w2_scales[0, q:16:4, :].bitcast(I32))
@@ -84,10 +84,9 @@ def tile_picked_embpos_none_po_kernel(
         w1c = keep.tile([P, H], U32, name="w1c", align_bytes=64)
         w1s = keep.tile([P, H], U8, name="w1s", align_bytes=64)
         w1b_v = w1b[:].rearrange("p (t m j) -> p m t j", t=PACK, j=PACK)
-        for a in range(2):
-            nc.scalar.copy(
-                w1b_v[:, 64 * a : 64 * (a + 1)], w1_raw[a][:].rearrange("p j (m t) -> p m t j", t=PACK)
-            )
+        w1_v = w1_raw[:].rearrange("p j (m t) -> p m t j", t=PACK)
+        nc.scalar.copy(w1b_v[:, 0:CAST_SPLIT], w1_v[:, 0:CAST_SPLIT])
+        nc.vector.tensor_copy(w1b_v[:, CAST_SPLIT:P], w1_v[:, CAST_SPLIT:P])
         nc.vector.quantize_mx(out=w1c[:].bitcast(FP8X4), scales=w1s[:], in_=w1b[:])
 
         def gather_words(c):

@@ -19,14 +19,18 @@ PACK = 4
 BLK = 128
 NBLK = S // BLK
 GATH = 256
-POS_CHUNKS = ((0, 256), (256, 512), (512, 1024))
-Y_CHUNKS = ((0, 256), (256, 512), (512, 640), (640, 768), (768, 896), (896, 1024))
-WORD_CHUNKS = ((0, 512), (512, 896), (896, 1024))
-VEC_ROUND = (3,)
-VEC_PSUM = (7,)
+KIB = 1024
 RUN = 2
 CAST_SPLIT = 48
-OUT_CHUNKS = ((0, 256), (256, 512), (512, 768), (768, 896), (896, 1024))
+POS_CHUNKS = ((0, 1), (1, 3), (3, 5), (5, 8))
+Y_CHUNKS = ((0, 1), (1, 2), (2, 4), (4, 5), (5, 6), (6, 7), (7, 8))
+Q_CHUNKS = ((0, 2), (2, 3), (3, 5), (5, 7), (7, 8))
+WORD_CHUNKS = ((0, 3), (3, 5), (5, 8))
+VEC_ROUND = (3, 4, 5, 6)
+
+
+def chunk_of(chunks, b):
+    return [n for n, (lo, hi) in enumerate(chunks) if lo <= b < hi][0]
 
 
 def tile_picked_embpos_none_po_kernel(
@@ -36,9 +40,17 @@ def tile_picked_embpos_none_po_kernel(
     add = mybir.AluOpType.add
     with ExitStack() as ctx:
         keep = ctx.enter_context(tc.tile_pool(name="keep", bufs=1))
+        lay = ctx.enter_context(tc.tile_pool(name="lay", bufs=1))
         ring = ctx.enter_context(tc.tile_pool(name="ring", bufs=3))
-        ps_h = ctx.enter_context(tc.psum_pool(name="ps_h", bufs=4))
-        ps_y = ctx.enter_context(tc.psum_pool(name="ps_y", bufs=4))
+        ps_h = ctx.enter_context(tc.psum_pool(name="ps_h", bufs=3))
+        ps_y = ctx.enter_context(tc.psum_pool(name="ps_y", bufs=5))
+
+        def laid(shape, dtype, name, kib):
+            return lay.tile(shape, dtype, name=name, offset=kib * KIB, align_bytes=64)
+
+        pos_at = [2 * lo for lo, hi in POS_CHUNKS]
+        w1b_at = 16
+        h_at = [20 + b for b in range(NBLK)]
 
         offsets = keep.tile([P, S // 16], U16, name="offsets")
         xw = keep.tile([P, T], I32, name="xw", align_bytes=64)
@@ -47,40 +59,37 @@ def tile_picked_embpos_none_po_kernel(
         w2w_raw = keep.tile([P, 2 * H], U8, name="w2w_raw", align_bytes=64)
         w1_raw = keep.tile([P, PACK, H], F32, name="w1_raw", align_bytes=64)
         pos_sb = [
-            keep.tile([P, PACK, b - a], F32, name=f"pos{a}", tag=f"slot{a}", align_bytes=64)
-            for a, b in POS_CHUNKS
+            laid([P, PACK, (hi - lo) * BLK], F32, f"pos{c}", pos_at[c]) for c, (lo, hi) in enumerate(POS_CHUNKS)
         ]
 
         nc.vector.memset(xs[:].bitcast(I32), 0)
         nc.vector.memset(w2s_raw[:].bitcast(I32), 0)
 
-        w1_rows = w1.rearrange("(p j) c -> p j c", j=PACK)
+        x_rows = x_words[0].rearrange("p n t -> p (n t)").bitcast(I32)
         pos_rows = pos.rearrange("(p t) n -> p t n", t=PACK)
         nc.sync.dma_start(w2w_raw[:].bitcast(I32), w2_words[0].bitcast(I32))
         nc.sync.dma_start(offsets[:], offs)
         for q in range(4):
             eng = nc.sync if q % 2 == 0 else nc.scalar
             eng.dma_start(xs[q:P:32, :].bitcast(I32), x_scales[0, q:16:4, :].bitcast(I32))
-        nc.sync.dma_start(w1_raw[:], w1_rows)
-        nc.sync.dma_start(xw[:], x_words[0].rearrange("p n t -> p (n t)").bitcast(I32))
+        nc.sync.dma_start(w1_raw[:], w1.rearrange("(p j) c -> p j c", j=PACK))
+        nc.sync.dma_start(xw[:], x_rows)
         for q in range(4):
             nc.sync.dma_start(w2s_raw[q:P:32, :].bitcast(I32), w2_scales[0, q:16:4, :].bitcast(I32))
-        for c, (a, b) in enumerate(POS_CHUNKS):
-            nc.sync.dma_start(pos_sb[c][:], pos_rows[:, :, a:b])
+        for c, (lo, hi) in enumerate(POS_CHUNKS):
+            nc.sync.dma_start(pos_sb[c][:], pos_rows[:, :, lo * BLK : hi * BLK])
 
         w2w = keep.tile([P, 2 * H], U8, name="w2w", align_bytes=64)
-        w2s = keep.tile([P, H], U8, name="w2s", align_bytes=64)
         nc.vector.tensor_copy(
             w2w[:].rearrange("p (t m e) -> p t m e", t=PACK, e=2),
             w2w_raw[:].rearrange("p (m t e) -> p t m e", t=PACK, e=2),
         )
 
         gs = [keep.tile([P, 512], U8, name=f"gs{c}", align_bytes=64) for c in range(2)]
-        gw = {}
         nc.vector.tensor_copy(gs[0][:], xs[:].indirect(offsets[:, 0:32]))
         nc.vector.tensor_copy(gs[1][:], xs[:].indirect(offsets[:, 32:64]))
 
-        w1b = keep.tile([P, PACK * H], BF16, name="w1b", align_bytes=64)
+        w1b = laid([P, PACK * H], BF16, "w1b", w1b_at)
         w1c = keep.tile([P, H], U32, name="w1c", align_bytes=64)
         w1s = keep.tile([P, H], U8, name="w1s", align_bytes=64)
         w1b_v = w1b[:].rearrange("p (t m j) -> p m t j", t=PACK, j=PACK)
@@ -89,28 +98,22 @@ def tile_picked_embpos_none_po_kernel(
         nc.vector.tensor_copy(w1b_v[:, CAST_SPLIT:P], w1_v[:, CAST_SPLIT:P])
         nc.vector.quantize_mx(out=w1c[:].bitcast(FP8X4), scales=w1s[:], in_=w1b[:])
 
-        def gather_words(c):
-            tag = f"gw{c}" if c < 2 else f"slot{POS_CHUNKS[c - 2][0]}"
-            gw[c] = keep.tile([P, GATH], U32, name=f"gw{c}", tag=tag, align_bytes=64)
+        gw = {}
+
+        def gather_words(c, kib):
+            gw[c] = laid([P, GATH], U32, f"gw{c}", kib)
             nc.vector.tensor_copy(
                 gw[c][:], xw[:].bitcast(U32).indirect(offsets[:, 16 * c : 16 * (c + 1)])
             )
 
-        gather_words(0)
-        gather_words(1)
-        nc.vector.tensor_copy(
-            w2s[:].rearrange("p (t m) -> p t m", t=PACK),
-            w2s_raw[:].rearrange("p (m t) -> p t m", t=PACK),
-        )
-
-        y_sb = [keep.tile([P, PACK, b - a], F32, name=f"y{a}", align_bytes=64) for a, b in Y_CHUNKS]
-        yb = [keep.tile([P, PACK * (b - a)], BF16, name=f"yb{a}", align_bytes=64) for a, b in OUT_CHUNKS]
-        yc = keep.tile([P, S], I32, name="yc", align_bytes=64)
+        y_sb = [
+            keep.tile([P, PACK, (hi - lo) * BLK], F32, name=f"y{lo}", align_bytes=64) for lo, hi in Y_CHUNKS
+        ]
         ys = keep.tile([P, S], U8, name="ys", align_bytes=64)
         out_rows = out_0.rearrange("(p t) n -> p t n", t=PACK)
         out_words = out_1[0].rearrange("p n t -> p (n t)").bitcast(I32)
-
-        acc_h, hb, hq, acc_y = {}, {}, {}, {}
+        late = {}
+        acc_h, hb, hq, acc_y, yb = {}, {}, {}, {}, {}
 
         def first_product(b):
             acc = ps_h.tile([P, PACK, BLK], F32, name="acc_h")
@@ -126,89 +129,111 @@ def tile_picked_embpos_none_po_kernel(
                     start=True,
                     stop=True,
                 )
-            return acc
+            acc_h[b] = acc
 
-        def add_pos(b, acc):
-            c = [n for n, (lo, hi) in enumerate(POS_CHUNKS) if lo <= b * BLK < hi][0]
-            o = b * BLK - POS_CHUNKS[c][0]
-            h16 = ring.tile([P, PACK * BLK], BF16, name="h16", align_bytes=64)
+        def add_pos(b):
+            c = chunk_of(POS_CHUNKS, b)
+            o = (b - POS_CHUNKS[c][0]) * BLK
+            hb[b] = laid([P, PACK * BLK], BF16, f"h{b}", h_at[b])
             nc.vector.tensor_tensor(
-                h16[:].rearrange("p (c i t) -> p c t i", i=RUN, t=PACK),
-                acc[:].rearrange("p t (c i) -> p c t i", i=RUN),
+                hb[b][:].rearrange("p (c i t) -> p c t i", i=RUN, t=PACK),
+                acc_h[b][:].rearrange("p t (c i) -> p c t i", i=RUN),
                 pos_sb[c][:, :, o : o + BLK].rearrange("p t (c i) -> p c t i", i=RUN),
                 add,
             )
-            return h16
 
-        def quant_h(h16):
+        def quant_h(b):
             hc = ring.tile([P, BLK], U32, name="hc", align_bytes=64)
             hs = ring.tile([P, BLK], U8, name="hs", align_bytes=64)
-            nc.vector.quantize_mx(out=hc[:].bitcast(FP8X4), scales=hs[:], in_=h16[:])
-            return hc, hs
+            nc.vector.quantize_mx(out=hc[:].bitcast(FP8X4), scales=hs[:], in_=hb[b][:])
+            hq[b] = hc, hs
 
-        def second_product(hc, hs):
+        def second_product(b):
+            hc, hs = hq[b]
             acc = ps_y.tile([P, PACK, BLK], F32, name="acc_y")
             for t in range(PACK):
                 nc.tensor.matmul_mx(
                     out=acc[:, t, :],
                     lhsT=w2w[:, 2 * t * P : 2 * (t + 1) * P].bitcast(FP4X4),
-                    lhsT_scale=w2s[:, t * P : (t + 1) * P],
+                    lhsT_scale=late["w2s"][:, t * P : (t + 1) * P],
                     rhs=hc[:].bitcast(FP8X4),
                     rhs_scale=hs[:],
                     start=True,
                     stop=True,
                 )
-            return acc
+            acc_y[b] = acc
 
-        def leave(b, acc):
-            c = [n for n, (lo, hi) in enumerate(OUT_CHUNKS) if lo <= b * BLK < hi][0]
-            o = b * BLK - OUT_CHUNKS[c][0]
-            dst = yb[c][:, PACK * o : PACK * (o + BLK)]
-            d = [n for n, (lo, hi) in enumerate(Y_CHUNKS) if lo <= b * BLK < hi][0]
+        def y_block(b):
+            d = chunk_of(Y_CHUNKS, b)
+            o = (b - Y_CHUNKS[d][0]) * BLK
+            return y_sb[d][:, :, o : o + BLK]
+
+        def leave(b):
+            nc.scalar.copy(y_block(b), acc_y[b][:])
+            d = chunk_of(Y_CHUNKS, b)
             lo, hi = Y_CHUNKS[d]
-            y_blk = y_sb[d][:, :, b * BLK - lo : (b + 1) * BLK - lo]
-            if b in VEC_PSUM:
-                nc.vector.tensor_copy(
-                    dst.rearrange("p (n t) -> p n t", t=PACK), acc[:].rearrange("p t n -> p n t")
-                )
-            elif b not in VEC_ROUND:
-                nc.scalar.copy(
-                    dst.rearrange("p (n t) -> p n t", t=PACK), acc[:].rearrange("p t n -> p n t")
-                )
-            nc.scalar.copy(y_blk, acc[:])
+            if b + 1 == hi:
+                nc.sync.dma_start(out_rows[:, :, lo * BLK : hi * BLK], y_sb[d][:])
+
+        def round_y(b):
+            c = chunk_of(Q_CHUNKS, b)
+            o = (b - Q_CHUNKS[c][0]) * BLK
+            dst = yb[c][:, PACK * o : PACK * (o + BLK)]
             if b in VEC_ROUND:
                 nc.vector.tensor_copy(
                     dst.rearrange("p (c i t) -> p c t i", i=RUN, t=PACK),
-                    y_blk.rearrange("p t (c i) -> p c t i", i=RUN),
+                    y_block(b).rearrange("p t (c i) -> p c t i", i=RUN),
                 )
-            if (b + 1) * BLK == hi:
-                nc.sync.dma_start(out_rows[:, :, lo:hi], y_sb[d][:])
+            else:
+                nc.scalar.copy(
+                    dst.rearrange("p (n t) -> p n t", t=PACK), acc_y[b][:].rearrange("p t n -> p n t")
+                )
 
         def quant_y(c):
-            lo, hi = OUT_CHUNKS[c]
+            lo, hi = Q_CHUNKS[c][0] * BLK, Q_CHUNKS[c][1] * BLK
+            yc = late["yc"]
             nc.vector.quantize_mx(out=yc[:, lo:hi].bitcast(FP8X4), scales=ys[:, lo:hi], in_=yb[c][:])
             for a, b in WORD_CHUNKS:
-                if b == hi:
-                    nc.sync.dma_start(out_words[:, a:b], yc[:, a:b])
+                if b * BLK == hi:
+                    nc.sync.dma_start(out_words[:, a * BLK : hi], yc[:, a * BLK : hi])
 
-        ends = {hi // BLK - 1: c for c, (lo, hi) in enumerate(OUT_CHUNKS)}
-        for s in range(NBLK + 4):
+        for c in (0, 1, 4):
+            lo, hi = Q_CHUNKS[c]
+            yb[c] = keep.tile([P, PACK * (hi - lo) * BLK], BF16, name=f"yb{c}", align_bytes=64)
+
+        for c in range(3):
+            gather_words(c, w1b_at + c)
+        for s in range(NBLK + 3):
             if s < NBLK:
-                acc_h[s] = first_product(s)
-            if s == 2:
-                hq[0] = quant_h(hb[0])
+                first_product(s)
             if 0 <= s - 1 < NBLK:
-                hb[s - 1] = add_pos(s - 1, acc_h[s - 1])
-            if 0 <= s - 2 < NBLK:
-                if s > 2:
-                    hq[s - 2] = quant_h(hb[s - 2])
-                acc_y[s - 2] = second_product(*hq[s - 2])
-            if s in (2, 4):
-                gather_words(s // 2 + 1)
+                add_pos(s - 1)
+            if s == 1:
+                late["w2s"] = laid([P, H], U8, "w2s", pos_at[0])
+                nc.vector.tensor_copy(
+                    late["w2s"][:].rearrange("p (t m) -> p t m", t=PACK),
+                    w2s_raw[:].rearrange("p (m t) -> p t m", t=PACK),
+                )
+                quant_h(0)
+                second_product(0)
+            if 1 <= s - 2 < NBLK:
+                quant_h(s - 2)
+                second_product(s - 2)
+            if s == 4:
+                gather_words(3, pos_at[1])
             if 0 <= s - 3 < NBLK:
-                leave(s - 3, acc_y[s - 3])
-            if s - 4 in ends:
-                quant_y(ends[s - 4])
+                leave(s - 3)
+            if 0 <= s - 4 < 3:
+                round_y(s - 4)
+
+        round_y(7)
+        late["yc"] = laid([P, S], I32, "yc", pos_at[3])
+        yb[2] = laid([P, PACK * 2 * BLK], BF16, "yb2", pos_at[3] + 4)
+        yb[3] = laid([P, PACK * 2 * BLK], BF16, "yb3", h_at[6])
+        for n, b in enumerate(VEC_ROUND):
+            round_y(b)
+            quant_y(n)
+        quant_y(4)
 
         for q in range(4):
             eng = nc.sync if q % 2 == 0 else nc.scalar

@@ -21,11 +21,10 @@ NBLK = S // BLK
 GATH = 256
 KIB = 1024
 RUN = 2
-CAST_SPLIT = 48
 POS_CHUNKS = ((0, 1), (1, 3), (3, 5), (5, 8))
-Y_CHUNKS = ((0, 1), (1, 2), (2, 4), (4, 5), (5, 6), (6, 7), (7, 8))
+Y_CHUNKS = ((0, 1), (1, 2), (2, 3), (3, 4), (4, 5), (5, 6), (6, 7), (7, 8))
 Q_CHUNKS = ((0, 2), (2, 3), (3, 5), (5, 7), (7, 8))
-WORD_CHUNKS = ((0, 3), (3, 5), (5, 8))
+WORD_CHUNKS = ((0, 3), (3, 8))
 VEC_ROUND = (3, 4, 5, 6)
 
 
@@ -57,7 +56,7 @@ def tile_picked_embpos_none_po_kernel(
         xs = keep.tile([P, T], U8, name="xs", align_bytes=64)
         w2s_raw = keep.tile([P, H], U8, name="w2s_raw", align_bytes=64)
         w2w_raw = keep.tile([P, 2 * H], U8, name="w2w_raw", align_bytes=64)
-        w1_raw = keep.tile([P, PACK, H], F32, name="w1_raw", align_bytes=64)
+        w1_raw = [keep.tile([P, PACK, H // 2], F32, name=f"w1_raw{a}", align_bytes=64) for a in range(2)]
         pos_sb = [
             laid([P, PACK, (hi - lo) * BLK], F32, f"pos{c}", pos_at[c]) for c, (lo, hi) in enumerate(POS_CHUNKS)
         ]
@@ -66,13 +65,15 @@ def tile_picked_embpos_none_po_kernel(
         nc.vector.memset(w2s_raw[:].bitcast(I32), 0)
 
         x_rows = x_words[0].rearrange("p n t -> p (n t)").bitcast(I32)
+        w1_rows = w1.rearrange("(p j) c -> p j c", j=PACK)
         pos_rows = pos.rearrange("(p t) n -> p t n", t=PACK)
         nc.sync.dma_start(w2w_raw[:].bitcast(I32), w2_words[0].bitcast(I32))
+        nc.sync.dma_start(w1_raw[0][:], w1_rows[:, :, 0 : H // 2])
         nc.sync.dma_start(offsets[:], offs)
         for q in range(4):
             eng = nc.sync if q % 2 == 0 else nc.scalar
             eng.dma_start(xs[q:P:32, :].bitcast(I32), x_scales[0, q:16:4, :].bitcast(I32))
-        nc.sync.dma_start(w1_raw[:], w1.rearrange("(p j) c -> p j c", j=PACK))
+        nc.sync.dma_start(w1_raw[1][:], w1_rows[:, :, H // 2 : H])
         nc.sync.dma_start(xw[:], x_rows)
         for q in range(4):
             nc.sync.dma_start(w2s_raw[q:P:32, :].bitcast(I32), w2_scales[0, q:16:4, :].bitcast(I32))
@@ -93,9 +94,10 @@ def tile_picked_embpos_none_po_kernel(
         w1c = keep.tile([P, H], U32, name="w1c", align_bytes=64)
         w1s = keep.tile([P, H], U8, name="w1s", align_bytes=64)
         w1b_v = w1b[:].rearrange("p (t m j) -> p m t j", t=PACK, j=PACK)
-        w1_v = w1_raw[:].rearrange("p j (m t) -> p m t j", t=PACK)
-        nc.scalar.copy(w1b_v[:, 0:CAST_SPLIT], w1_v[:, 0:CAST_SPLIT])
-        nc.vector.tensor_copy(w1b_v[:, CAST_SPLIT:P], w1_v[:, CAST_SPLIT:P])
+        for a in range(2):
+            nc.scalar.copy(
+                w1b_v[:, 64 * a : 64 * (a + 1)], w1_raw[a][:].rearrange("p j (m t) -> p m t j", t=PACK)
+            )
         nc.vector.quantize_mx(out=w1c[:].bitcast(FP8X4), scales=w1s[:], in_=w1b[:])
 
         gw = {}
@@ -230,9 +232,13 @@ def tile_picked_embpos_none_po_kernel(
         late["yc"] = laid([P, S], I32, "yc", pos_at[3])
         yb[2] = laid([P, PACK * 2 * BLK], BF16, "yb2", pos_at[3] + 4)
         yb[3] = laid([P, PACK * 2 * BLK], BF16, "yb3", h_at[6])
-        for n, b in enumerate(VEC_ROUND):
+        quant_y(0)
+        quant_y(1)
+        for b in VEC_ROUND[:3]:
             round_y(b)
-            quant_y(n)
+        quant_y(2)
+        round_y(VEC_ROUND[3])
+        quant_y(3)
         quant_y(4)
 
         for q in range(4):

@@ -48,15 +48,15 @@ def tile_picked_embpos_none_po_kernel(
             return lay.tile(shape, dtype, name=name, offset=kib * KIB, align_bytes=64)
 
         pos_at = [2 * lo for lo, hi in POS_CHUNKS]
-        w1b_at = 16
-        h_at = [20 + b for b in range(NBLK)]
+        w1_at = 16
+        h_at = [24 + b for b in range(NBLK)]
 
         offsets = keep.tile([P, S // 16], U16, name="offsets")
         xw = keep.tile([P, T], I32, name="xw", align_bytes=64)
         xs = keep.tile([P, T], U8, name="xs", align_bytes=64)
         w2s_raw = keep.tile([P, H], U8, name="w2s_raw", align_bytes=64)
         w2w_raw = keep.tile([P, 2 * H], U8, name="w2w_raw", align_bytes=64)
-        w1_raw = [keep.tile([P, PACK, H // 2], F32, name=f"w1_raw{a}", align_bytes=64) for a in range(2)]
+        w1_raw = [laid([P, PACK, H // 2], F32, f"w1_raw{a}", w1_at + 4 * a) for a in range(2)]
         pos_sb = [
             laid([P, PACK, (hi - lo) * BLK], F32, f"pos{c}", pos_at[c]) for c, (lo, hi) in enumerate(POS_CHUNKS)
         ]
@@ -67,7 +67,6 @@ def tile_picked_embpos_none_po_kernel(
         x_rows = x_words[0].rearrange("p n t -> p (n t)").bitcast(I32)
         w1_rows = w1.rearrange("(p j) c -> p j c", j=PACK)
         pos_rows = pos.rearrange("(p t) n -> p t n", t=PACK)
-        nc.sync.dma_start(w2w_raw[:].bitcast(I32), w2_words[0].bitcast(I32))
         nc.sync.dma_start(w1_raw[0][:], w1_rows[:, :, 0 : H // 2])
         nc.sync.dma_start(offsets[:], offs)
         for q in range(4):
@@ -75,13 +74,14 @@ def tile_picked_embpos_none_po_kernel(
             eng.dma_start(xs[q:P:32, :].bitcast(I32), x_scales[0, q:16:4, :].bitcast(I32))
         nc.sync.dma_start(w1_raw[1][:], w1_rows[:, :, H // 2 : H])
         nc.sync.dma_start(xw[:], x_rows)
+        nc.sync.dma_start(w2w_raw[:].bitcast(I32), w2_words[0].bitcast(I32))
         for q in range(4):
             nc.sync.dma_start(w2s_raw[q:P:32, :].bitcast(I32), w2_scales[0, q:16:4, :].bitcast(I32))
         for c, (lo, hi) in enumerate(POS_CHUNKS):
             nc.sync.dma_start(pos_sb[c][:], pos_rows[:, :, lo * BLK : hi * BLK])
 
         w2w = keep.tile([P, 2 * H], U8, name="w2w", align_bytes=64)
-        nc.vector.tensor_copy(
+        nc.gpsimd.tensor_copy(
             w2w[:].rearrange("p (t m e) -> p t m e", t=PACK, e=2),
             w2w_raw[:].rearrange("p (m t e) -> p t m e", t=PACK, e=2),
         )
@@ -90,7 +90,7 @@ def tile_picked_embpos_none_po_kernel(
         nc.vector.tensor_copy(gs[0][:], xs[:].indirect(offsets[:, 0:32]))
         nc.vector.tensor_copy(gs[1][:], xs[:].indirect(offsets[:, 32:64]))
 
-        w1b = laid([P, PACK * H], BF16, "w1b", w1b_at)
+        w1b = keep.tile([P, PACK * H], BF16, name="w1b", align_bytes=64)
         w1c = keep.tile([P, H], U32, name="w1c", align_bytes=64)
         w1s = keep.tile([P, H], U8, name="w1s", align_bytes=64)
         w1b_v = w1b[:].rearrange("p (t m j) -> p m t j", t=PACK, j=PACK)
@@ -204,7 +204,7 @@ def tile_picked_embpos_none_po_kernel(
             yb[c] = keep.tile([P, PACK * (hi - lo) * BLK], BF16, name=f"yb{c}", align_bytes=64)
 
         for c in range(3):
-            gather_words(c, w1b_at + c)
+            gather_words(c, w1_at + 4 + c)
         for s in range(NBLK + 3):
             if s < NBLK:
                 first_product(s)

@@ -21,6 +21,9 @@ NBLK = S // BLK
 GATH = 256
 KIB = 1024
 RUN = 2
+W1_FIRST = 224
+W1_PIECES = ((0, W1_FIRST), (W1_FIRST, H))
+CAST_POOL = 24
 POS_CHUNKS = ((0, 1), (1, 3), (3, 5), (5, 8))
 Y_CHUNKS = ((0, 1), (1, 2), (2, 3), (3, 4), (4, 5), (5, 6), (6, 7), (7, 8))
 Q_CHUNKS = ((0, 2), (2, 3), (3, 5), (5, 7), (7, 8))
@@ -49,14 +52,16 @@ def tile_picked_embpos_none_po_kernel(
 
         pos_at = [2 * lo for lo, hi in POS_CHUNKS]
         w1_at = 16
-        h_at = [24 + b for b in range(NBLK)]
+        h_at = [25 + b for b in range(NBLK)]
 
         offsets = keep.tile([P, S // 16], U16, name="offsets")
         xw = keep.tile([P, T], I32, name="xw", align_bytes=64)
         xs = keep.tile([P, T], U8, name="xs", align_bytes=64)
         w2s_raw = keep.tile([P, H], U8, name="w2s_raw", align_bytes=64)
         w2w_raw = keep.tile([P, 2 * H], U8, name="w2w_raw", align_bytes=64)
-        w1_raw = [laid([P, PACK, H // 2], F32, f"w1_raw{a}", w1_at + 4 * a) for a in range(2)]
+        w1_raw = [
+            laid([P, PACK, hi - lo], F32, f"w1_raw{a}", w1_at + 4 * a) for a, (lo, hi) in enumerate(W1_PIECES)
+        ]
         pos_sb = [
             laid([P, PACK, (hi - lo) * BLK], F32, f"pos{c}", pos_at[c]) for c, (lo, hi) in enumerate(POS_CHUNKS)
         ]
@@ -67,12 +72,12 @@ def tile_picked_embpos_none_po_kernel(
         x_rows = x_words[0].rearrange("p n t -> p (n t)").bitcast(I32)
         w1_rows = w1.rearrange("(p j) c -> p j c", j=PACK)
         pos_rows = pos.rearrange("(p t) n -> p t n", t=PACK)
-        nc.sync.dma_start(w1_raw[0][:], w1_rows[:, :, 0 : H // 2])
+        nc.sync.dma_start(w1_raw[0][:], w1_rows[:, :, 0:W1_FIRST])
         nc.sync.dma_start(offsets[:], offs)
         for q in range(4):
             eng = nc.sync if q % 2 == 0 else nc.scalar
             eng.dma_start(xs[q:P:32, :].bitcast(I32), x_scales[0, q:16:4, :].bitcast(I32))
-        nc.sync.dma_start(w1_raw[1][:], w1_rows[:, :, H // 2 : H])
+        nc.sync.dma_start(w1_raw[1][:], w1_rows[:, :, W1_FIRST:H])
         nc.sync.dma_start(xw[:], x_rows)
         nc.sync.dma_start(w2w_raw[:].bitcast(I32), w2_words[0].bitcast(I32))
         for q in range(4):
@@ -80,25 +85,31 @@ def tile_picked_embpos_none_po_kernel(
         for c, (lo, hi) in enumerate(POS_CHUNKS):
             nc.sync.dma_start(pos_sb[c][:], pos_rows[:, :, lo * BLK : hi * BLK])
 
+        gs = keep.tile([P, S], U8, name="gs", align_bytes=64)
+        nc.vector.tensor_copy(gs[:], xs[:].indirect(offsets[:]))
+
+        w1b = keep.tile([P, PACK * H], BF16, name="w1b", align_bytes=64)
+        w1c = keep.tile([P, H], U32, name="w1c", align_bytes=64)
+        w1s = keep.tile([P, H], U8, name="w1s", align_bytes=64)
+        w1b_v = w1b[:].rearrange("p (t m j) -> p m t j", t=PACK, j=PACK)
+        w1_v = [raw[:].rearrange("p j (m t) -> p m t j", t=PACK) for raw in w1_raw]
+        m_first, m_cut = W1_FIRST // PACK, P - CAST_POOL
+        nc.scalar.copy(w1b_v[:, 0:m_first], w1_v[0])
+        nc.scalar.copy(w1b_v[:, m_first:m_cut], w1_v[1][:, 0 : m_cut - m_first])
+        nc.gpsimd.tensor_copy(w1b_v[:, m_cut:P], w1_v[1][:, m_cut - m_first : P - m_first])
+        nc.vector.quantize_mx(out=w1c[:].bitcast(FP8X4), scales=w1s[:], in_=w1b[:])
+
         w2w = keep.tile([P, 2 * H], U8, name="w2w", align_bytes=64)
         nc.gpsimd.tensor_copy(
             w2w[:].rearrange("p (t m e) -> p t m e", t=PACK, e=2),
             w2w_raw[:].rearrange("p (m t e) -> p t m e", t=PACK, e=2),
         )
 
-        gs = [keep.tile([P, 512], U8, name=f"gs{c}", align_bytes=64) for c in range(2)]
-        nc.vector.tensor_copy(gs[0][:], xs[:].indirect(offsets[:, 0:32]))
-        nc.vector.tensor_copy(gs[1][:], xs[:].indirect(offsets[:, 32:64]))
-
-        w1b = keep.tile([P, PACK * H], BF16, name="w1b", align_bytes=64)
-        w1c = keep.tile([P, H], U32, name="w1c", align_bytes=64)
-        w1s = keep.tile([P, H], U8, name="w1s", align_bytes=64)
-        w1b_v = w1b[:].rearrange("p (t m j) -> p m t j", t=PACK, j=PACK)
-        for a in range(2):
-            nc.scalar.copy(
-                w1b_v[:, 64 * a : 64 * (a + 1)], w1_raw[a][:].rearrange("p j (m t) -> p m t j", t=PACK)
-            )
-        nc.vector.quantize_mx(out=w1c[:].bitcast(FP8X4), scales=w1s[:], in_=w1b[:])
+        w2s = keep.tile([P, H], U8, name="w2s", align_bytes=64)
+        nc.gpsimd.tensor_copy(
+            w2s[:].rearrange("p (t m) -> p t m", t=PACK),
+            w2s_raw[:].rearrange("p (m t) -> p t m", t=PACK),
+        )
 
         gw = {}
 
@@ -120,14 +131,13 @@ def tile_picked_embpos_none_po_kernel(
         def first_product(b):
             acc = ps_h.tile([P, PACK, BLK], F32, name="acc_h")
             g, o = divmod(b * BLK, GATH)
-            g2, o2 = divmod(b * BLK, 512)
             for t in range(PACK):
                 nc.tensor.matmul_mx(
                     out=acc[:, t, :],
                     lhsT=w1c[:, t * P : (t + 1) * P].bitcast(FP8X4),
                     lhsT_scale=w1s[:, t * P : (t + 1) * P],
                     rhs=gw[g][:, o : o + BLK].bitcast(FP8X4),
-                    rhs_scale=gs[g2][:, o2 : o2 + BLK],
+                    rhs_scale=gs[:, b * BLK : (b + 1) * BLK],
                     start=True,
                     stop=True,
                 )
@@ -157,7 +167,7 @@ def tile_picked_embpos_none_po_kernel(
                 nc.tensor.matmul_mx(
                     out=acc[:, t, :],
                     lhsT=w2w[:, 2 * t * P : 2 * (t + 1) * P].bitcast(FP4X4),
-                    lhsT_scale=late["w2s"][:, t * P : (t + 1) * P],
+                    lhsT_scale=w2s[:, t * P : (t + 1) * P],
                     rhs=hc[:].bitcast(FP8X4),
                     rhs_scale=hs[:],
                     start=True,
@@ -211,11 +221,6 @@ def tile_picked_embpos_none_po_kernel(
             if 0 <= s - 1 < NBLK:
                 add_pos(s - 1)
             if s == 1:
-                late["w2s"] = laid([P, H], U8, "w2s", pos_at[0])
-                nc.vector.tensor_copy(
-                    late["w2s"][:].rearrange("p (t m) -> p t m", t=PACK),
-                    w2s_raw[:].rearrange("p (m t) -> p t m", t=PACK),
-                )
                 quant_h(0)
                 second_product(0)
             if 1 <= s - 2 < NBLK:

@@ -18,17 +18,13 @@ P = 128
 PACK = 4
 BLK = 128
 NBLK = S // BLK
-GATH = 256
-KIB = 1024
+QUARTER = 256
+BANK = 2048
 RUN = 2
 W1_FIRST = 224
 W1_PIECES = ((0, W1_FIRST), (W1_FIRST, H))
 CAST_POOL = 24
-POS_CHUNKS = ((0, 1), (1, 3), (3, 5), (5, 8))
-Y_CHUNKS = ((0, 1), (1, 2), (2, 3), (3, 4), (4, 5), (5, 6), (6, 7), (7, 8))
-Q_CHUNKS = ((0, 2), (2, 3), (3, 5), (5, 7), (7, 8))
-WORD_CHUNKS = ((0, 3), (3, 8))
-VEC_ROUND = (3, 4, 5, 6)
+POS_CHUNKS = ((0, 1), (1, 2), (2, 3), (3, 5), (5, 8))
 
 
 def chunk_of(chunks, b):
@@ -43,25 +39,26 @@ def tile_picked_embpos_none_po_kernel(
     with ExitStack() as ctx:
         keep = ctx.enter_context(tc.tile_pool(name="keep", bufs=1))
         lay = ctx.enter_context(tc.tile_pool(name="lay", bufs=1))
-        ring = ctx.enter_context(tc.tile_pool(name="ring", bufs=3))
-        ps_h = ctx.enter_context(tc.psum_pool(name="ps_h", bufs=3))
+        ps_h = ctx.enter_context(tc.psum_pool(name="ps_h", bufs=1))
         ps_y = ctx.enter_context(tc.psum_pool(name="ps_y", bufs=5))
 
-        def laid(shape, dtype, name, kib):
-            return lay.tile(shape, dtype, name=name, offset=kib * KIB, align_bytes=64)
+        def laid(shape, dtype, name, at):
+            return lay.tile(shape, dtype, name=name, offset=at * QUARTER, align_bytes=64)
 
-        pos_at = [2 * lo for lo, hi in POS_CHUNKS]
-        w1_at = 16
-        h_at = [25 + b for b in range(NBLK)]
+        w1_at = (0, 16)
+        pos_at = (36, 44, 52, 60, 76)
+        h_at = {b: 100 + 4 * b for b in range(NBLK)}
+        words_at = {0: 16, 1: 18, 6: 22, 3: 16, 4: h_at[0], 5: h_at[1]}
+        yb_at = {0: 132, 2: 140, 3: pos_at[4] + 12, 4: pos_at[4], 6: pos_at[4] + 8, 7: 148}
+        yc_at = pos_at[3]
+        bank_of = {b: b % 3 for b in range(NBLK)}
 
         offsets = keep.tile([P, S // 16], U16, name="offsets")
         xw = keep.tile([P, T], I32, name="xw", align_bytes=64)
         xs = keep.tile([P, T], U8, name="xs", align_bytes=64)
         w2s_raw = keep.tile([P, H], U8, name="w2s_raw", align_bytes=64)
         w2w_raw = keep.tile([P, 2 * H], U8, name="w2w_raw", align_bytes=64)
-        w1_raw = [
-            laid([P, PACK, hi - lo], F32, f"w1_raw{a}", w1_at + 4 * a) for a, (lo, hi) in enumerate(W1_PIECES)
-        ]
+        w1_raw = [laid([P, PACK, hi - lo], F32, f"w1_raw{a}", w1_at[a]) for a, (lo, hi) in enumerate(W1_PIECES)]
         pos_sb = [
             laid([P, PACK, (hi - lo) * BLK], F32, f"pos{c}", pos_at[c]) for c, (lo, hi) in enumerate(POS_CHUNKS)
         ]
@@ -79,11 +76,17 @@ def tile_picked_embpos_none_po_kernel(
             eng.dma_start(xs[q:P:32, :].bitcast(I32), x_scales[0, q:16:4, :].bitcast(I32))
         nc.sync.dma_start(w1_raw[1][:], w1_rows[:, :, W1_FIRST:H])
         nc.sync.dma_start(xw[:], x_rows)
-        nc.sync.dma_start(w2w_raw[:].bitcast(I32), w2_words[0].bitcast(I32))
+
+        def load_pos(c):
+            lo, hi = POS_CHUNKS[c]
+            nc.sync.dma_start(pos_sb[c][:], pos_rows[:, :, lo * BLK : hi * BLK])
+
+        load_pos(0)
         for q in range(4):
             nc.sync.dma_start(w2s_raw[q:P:32, :].bitcast(I32), w2_scales[0, q:16:4, :].bitcast(I32))
-        for c, (lo, hi) in enumerate(POS_CHUNKS):
-            nc.sync.dma_start(pos_sb[c][:], pos_rows[:, :, lo * BLK : hi * BLK])
+        nc.sync.dma_start(w2w_raw[:].bitcast(I32), w2_words[0].bitcast(I32))
+        for c in range(1, len(POS_CHUNKS)):
+            load_pos(c)
 
         gs = keep.tile([P, S], U8, name="gs", align_bytes=64)
         nc.vector.tensor_copy(gs[:], xs[:].indirect(offsets[:]))
@@ -100,65 +103,69 @@ def tile_picked_embpos_none_po_kernel(
         nc.vector.quantize_mx(out=w1c[:].bitcast(FP8X4), scales=w1s[:], in_=w1b[:])
 
         w2w = keep.tile([P, 2 * H], U8, name="w2w", align_bytes=64)
-        nc.gpsimd.tensor_copy(
-            w2w[:].rearrange("p (t m e) -> p t m e", t=PACK, e=2),
-            w2w_raw[:].rearrange("p (m t e) -> p t m e", t=PACK, e=2),
+        nc.scalar.copy(
+            w2w[:].bitcast(U16).rearrange("p (t m) -> p t m", t=PACK),
+            w2w_raw[:].bitcast(U16).rearrange("p (m t) -> p t m", t=PACK),
         )
-
         w2s = keep.tile([P, H], U8, name="w2s", align_bytes=64)
         nc.gpsimd.tensor_copy(
             w2s[:].rearrange("p (t m) -> p t m", t=PACK),
             w2s_raw[:].rearrange("p (m t) -> p t m", t=PACK),
         )
 
-        gw = {}
-
-        def gather_words(c, kib):
-            gw[c] = laid([P, GATH], U32, f"gw{c}", kib)
-            nc.vector.tensor_copy(
-                gw[c][:], xw[:].bitcast(U32).indirect(offsets[:, 16 * c : 16 * (c + 1)])
-            )
-
-        y_sb = [
-            keep.tile([P, PACK, (hi - lo) * BLK], F32, name=f"y{lo}", align_bytes=64) for lo, hi in Y_CHUNKS
-        ]
         ys = keep.tile([P, S], U8, name="ys", align_bytes=64)
         out_rows = out_0.rearrange("(p t) n -> p t n", t=PACK)
         out_words = out_1[0].rearrange("p n t -> p (n t)").bitcast(I32)
-        late = {}
-        acc_h, hb, hq, acc_y, yb = {}, {}, {}, {}, {}
+        gw, acc_h, hb, hq, acc_y, y_sb, yb, late = {}, {}, {}, {}, {}, {}, {}, {}
+
+        def cols(b, n=1):
+            return slice(b * BLK, (b + n) * BLK)
+
+        def gather_words(b, n=1):
+            g = laid([P, n * BLK], U32, f"gw{b}", words_at[b])
+            per = BLK // 16
+            nc.vector.tensor_copy(g[:], xw[:].bitcast(U32).indirect(offsets[:, per * b : per * (b + n)]))
+            for i in range(n):
+                gw[b + i] = g[:, cols(i)]
 
         def first_product(b):
-            acc = ps_h.tile([P, PACK, BLK], F32, name="acc_h")
-            g, o = divmod(b * BLK, GATH)
+            acc = ps_h.tile([P, PACK, BLK], F32, name=f"acc_h{b}", offset=bank_of[b] * BANK)
             for t in range(PACK):
                 nc.tensor.matmul_mx(
                     out=acc[:, t, :],
                     lhsT=w1c[:, t * P : (t + 1) * P].bitcast(FP8X4),
                     lhsT_scale=w1s[:, t * P : (t + 1) * P],
-                    rhs=gw[g][:, o : o + BLK].bitcast(FP8X4),
-                    rhs_scale=gs[:, b * BLK : (b + 1) * BLK],
+                    rhs=gw[b].bitcast(FP8X4),
+                    rhs_scale=gs[:, cols(b)],
                     start=True,
                     stop=True,
                 )
             acc_h[b] = acc
 
-        def add_pos(b):
+        def pos_block(b):
             c = chunk_of(POS_CHUNKS, b)
-            o = (b - POS_CHUNKS[c][0]) * BLK
-            hb[b] = laid([P, PACK * BLK], BF16, f"h{b}", h_at[b])
+            return pos_sb[c][:, :, cols(b - POS_CHUNKS[c][0])]
+
+        def new_h(b, n=1):
+            tile = laid([P, n * PACK * BLK], BF16, f"h{b}", h_at[b])
+            for i in range(n):
+                hb[b + i] = tile[:, i * PACK * BLK : (i + 1) * PACK * BLK]
+            hb[b, n] = tile
+
+        def add_pos(b):
             nc.vector.tensor_tensor(
-                hb[b][:].rearrange("p (c i t) -> p c t i", i=RUN, t=PACK),
+                hb[b].rearrange("p (c i t) -> p c t i", i=RUN, t=PACK),
                 acc_h[b][:].rearrange("p t (c i) -> p c t i", i=RUN),
-                pos_sb[c][:, :, o : o + BLK].rearrange("p t (c i) -> p c t i", i=RUN),
+                pos_block(b).rearrange("p t (c i) -> p c t i", i=RUN),
                 add,
             )
 
-        def quant_h(b):
-            hc = ring.tile([P, BLK], U32, name="hc", align_bytes=64)
-            hs = ring.tile([P, BLK], U8, name="hs", align_bytes=64)
-            nc.vector.quantize_mx(out=hc[:].bitcast(FP8X4), scales=hs[:], in_=hb[b][:])
-            hq[b] = hc, hs
+        def quant_h(b, n=1):
+            hc = keep.tile([P, n * BLK], U32, name=f"hc{b}", align_bytes=64)
+            hs = keep.tile([P, n * BLK], U8, name=f"hs{b}", align_bytes=64)
+            nc.vector.quantize_mx(out=hc[:].bitcast(FP8X4), scales=hs[:], in_=hb[b, n][:])
+            for i in range(n):
+                hq[b + i] = hc[:, cols(i)], hs[:, cols(i)]
 
         def second_product(b):
             hc, hs = hq[b]
@@ -168,83 +175,98 @@ def tile_picked_embpos_none_po_kernel(
                     out=acc[:, t, :],
                     lhsT=w2w[:, 2 * t * P : 2 * (t + 1) * P].bitcast(FP4X4),
                     lhsT_scale=w2s[:, t * P : (t + 1) * P],
-                    rhs=hc[:].bitcast(FP8X4),
-                    rhs_scale=hs[:],
+                    rhs=hc.bitcast(FP8X4),
+                    rhs_scale=hs,
                     start=True,
                     stop=True,
                 )
             acc_y[b] = acc
 
-        def y_block(b):
-            d = chunk_of(Y_CHUNKS, b)
-            o = (b - Y_CHUNKS[d][0]) * BLK
-            return y_sb[d][:, :, o : o + BLK]
-
         def leave(b):
-            nc.scalar.copy(y_block(b), acc_y[b][:])
-            d = chunk_of(Y_CHUNKS, b)
-            lo, hi = Y_CHUNKS[d]
-            if b + 1 == hi:
-                nc.sync.dma_start(out_rows[:, :, lo * BLK : hi * BLK], y_sb[d][:])
+            y_sb[b] = keep.tile([P, PACK, BLK], F32, name=f"y{b}", align_bytes=64)
+            nc.scalar.copy(y_sb[b][:], acc_y[b][:])
+            nc.sync.dma_start(out_rows[:, :, cols(b)], y_sb[b][:])
 
-        def round_y(b):
-            c = chunk_of(Q_CHUNKS, b)
-            o = (b - Q_CHUNKS[c][0]) * BLK
-            dst = yb[c][:, PACK * o : PACK * (o + BLK)]
-            if b in VEC_ROUND:
-                nc.vector.tensor_copy(
-                    dst.rearrange("p (c i t) -> p c t i", i=RUN, t=PACK),
-                    y_block(b).rearrange("p t (c i) -> p c t i", i=RUN),
-                )
-            else:
-                nc.scalar.copy(
-                    dst.rearrange("p (n t) -> p n t", t=PACK), acc_y[b][:].rearrange("p t n -> p n t")
-                )
+        def new_yb(b, n=1):
+            tile = laid([P, n * PACK * BLK], BF16, f"yb{b}", yb_at[b])
+            for i in range(n):
+                yb[b + i] = tile[:, i * PACK * BLK : (i + 1) * PACK * BLK]
+            yb[b, n] = tile
 
-        def quant_y(c):
-            lo, hi = Q_CHUNKS[c][0] * BLK, Q_CHUNKS[c][1] * BLK
-            yc = late["yc"]
-            nc.vector.quantize_mx(out=yc[:, lo:hi].bitcast(FP8X4), scales=ys[:, lo:hi], in_=yb[c][:])
-            for a, b in WORD_CHUNKS:
-                if b * BLK == hi:
-                    nc.sync.dma_start(out_words[:, a * BLK : hi], yc[:, a * BLK : hi])
+        def round_scalar(b):
+            nc.scalar.copy(yb[b].rearrange("p (n t) -> p n t", t=PACK), acc_y[b][:].rearrange("p t n -> p n t"))
 
-        for c in (0, 1, 4):
-            lo, hi = Q_CHUNKS[c]
-            yb[c] = keep.tile([P, PACK * (hi - lo) * BLK], BF16, name=f"yb{c}", align_bytes=64)
+        def round_vector(b):
+            nc.vector.tensor_copy(
+                yb[b].rearrange("p (c i t) -> p c t i", i=RUN, t=PACK),
+                y_sb[b][:].rearrange("p t (c i) -> p c t i", i=RUN),
+            )
 
-        for c in range(3):
-            gather_words(c, w1_at + 4 + c)
-        for s in range(NBLK + 3):
-            if s < NBLK:
-                first_product(s)
-            if 0 <= s - 1 < NBLK:
-                add_pos(s - 1)
-            if s == 1:
-                quant_h(0)
-                second_product(0)
-            if 1 <= s - 2 < NBLK:
-                quant_h(s - 2)
-                second_product(s - 2)
-            if s == 4:
-                gather_words(3, pos_at[1])
-            if 0 <= s - 3 < NBLK:
-                leave(s - 3)
-            if 0 <= s - 4 < 3:
-                round_y(s - 4)
+        def quant_y(b, n=1):
+            nc.vector.quantize_mx(
+                out=late["yc"][:, cols(b, n)].bitcast(FP8X4), scales=ys[:, cols(b, n)], in_=yb[b, n][:]
+            )
 
-        round_y(7)
-        late["yc"] = laid([P, S], I32, "yc", pos_at[3])
-        yb[2] = laid([P, PACK * 2 * BLK], BF16, "yb2", pos_at[3] + 4)
-        yb[3] = laid([P, PACK * 2 * BLK], BF16, "yb3", h_at[6])
-        quant_y(0)
-        quant_y(1)
-        for b in VEC_ROUND[:3]:
-            round_y(b)
+        def store_words(b, n):
+            nc.sync.dma_start(out_words[:, cols(b, n)], late["yc"][:, cols(b, n)])
+
+        def add_block(b):
+            new_h(b)
+            add_pos(b)
+
+        def second_layer(b):
+            quant_h(b)
+            second_product(b)
+            leave(b)
+
+        gather_words(0)
+        first_product(0)
+        gather_words(1, 2)
+        first_product(1)
+        first_product(2)
+        gather_words(6, 2)
+        new_yb(0, 2)
+        new_yb(2)
+        for b in (0, 1, 2):
+            add_block(b)
+            gather_words(b + 3)
+            quant_h(b)
+            second_product(b)
+            first_product(b + 3)
+            leave(b)
+            round_scalar(b)
+
+        add_block(3)
+        first_product(6)
+        add_block(4)
+        first_product(7)
+        second_layer(3)
+        add_block(5)
+        second_layer(4)
+        late["yc"] = laid([P, S], I32, "yc", yc_at)
+        quant_y(0, 2)
+        store_words(0, 2)
+        add_block(6)
+        second_layer(5)
+        add_block(7)
+        second_layer(6)
+        second_layer(7)
+        new_yb(7)
+        round_scalar(7)
+
         quant_y(2)
-        round_y(VEC_ROUND[3])
+        new_yb(3)
+        new_yb(4, 2)
+        new_yb(6)
+        for b in (3, 4, 5):
+            round_vector(b)
         quant_y(3)
-        quant_y(4)
+        round_vector(6)
+        quant_y(4, 2)
+        store_words(2, 4)
+        quant_y(6)
+        quant_y(7)
+        store_words(6, 2)
 
         for q in range(4):
             eng = nc.sync if q % 2 == 0 else nc.scalar

@@ -24,7 +24,7 @@ RUN = 2
 W1_FIRST = 224
 W1_PIECES = ((0, W1_FIRST), (W1_FIRST, H))
 CAST_POOL = 24
-POS_CHUNKS = ((0, 1), (1, 2), (2, 3), (3, 5), (5, 8))
+POS_CHUNKS = ((0, 1), (1, 3), (3, 6), (6, 8))
 
 
 def chunk_of(chunks, b):
@@ -46,11 +46,11 @@ def tile_picked_embpos_none_po_kernel(
             return lay.tile(shape, dtype, name=name, offset=at * QUARTER, align_bytes=64)
 
         w1_at = (0, 16)
-        pos_at = (36, 44, 52, 60, 76)
-        h_at = {b: 100 + 4 * b for b in range(NBLK)}
-        words_at = {0: 16, 1: 18, 6: 22, 3: 16, 4: h_at[0], 5: h_at[1]}
-        yb_at = {0: 132, 2: 140, 3: pos_at[4] + 12, 4: pos_at[4], 6: pos_at[4] + 8, 7: 148}
-        yc_at = pos_at[3]
+        pos_at = (36, 44, 60, 84)
+        h_at = {b: pos_at[0] if b == 1 else 100 + 4 * b for b in range(NBLK)}
+        words_at = {0: 16, 1: 18, 4: 22, 3: 16}
+        yb_at = {0: 132, 2: 140, 3: pos_at[3] + 12, 4: pos_at[3], 6: pos_at[3] + 8, 7: 148}
+        yc_at = pos_at[2]
         bank_of = {b: b % 3 for b in range(NBLK)}
 
         offsets = keep.tile([P, S // 16], U16, name="offsets")
@@ -224,23 +224,24 @@ def tile_picked_embpos_none_po_kernel(
         gather_words(1, 2)
         first_product(1)
         first_product(2)
-        gather_words(6, 2)
+        gather_words(4, 4)
         new_yb(0, 2)
         new_yb(2)
-        for b in (0, 1, 2):
+        add_block(0)
+        gather_words(3)
+        quant_h(0)
+        second_product(0)
+        first_product(3)
+        leave(0)
+        round_scalar(0)
+        add_block(1)
+        first_product(4)
+        for b in (2, 3, 4):
             add_block(b)
-            gather_words(b + 3)
-            quant_h(b)
-            second_product(b)
             first_product(b + 3)
-            leave(b)
-            round_scalar(b)
-
-        add_block(3)
-        first_product(6)
-        add_block(4)
-        first_product(7)
-        second_layer(3)
+            second_layer(b - 1)
+            if b < 4:
+                round_scalar(b - 1)
         add_block(5)
         second_layer(4)
         late["yc"] = laid([P, S], I32, "yc", yc_at)

@@ -113,7 +113,7 @@ def tile_picked_embpos_none_po_kernel(
             w2s_raw[:].rearrange("p (m t) -> p t m", t=PACK),
         )
 
-        ys = keep.tile([P, S], U8, name="ys", align_bytes=64)
+        ys = keep.tile([P, 2 * BLK], U8, name="ys", align_bytes=64)
         out_rows = out_0.rearrange("(p t) n -> p t n", t=PACK)
         out_words = out_1[0].rearrange("p n t -> p (n t)").bitcast(I32)
         gw, acc_h, hb, hq, acc_y, y_sb, yb, late = {}, {}, {}, {}, {}, {}, {}, {}
@@ -204,7 +204,9 @@ def tile_picked_embpos_none_po_kernel(
 
         def quant_y(b, n=1):
             nc.vector.quantize_mx(
-                out=late["yc"][:, cols(b, n)].bitcast(FP8X4), scales=ys[:, cols(b, n)], in_=yb[b, n][:]
+                out=late["yc"][:, cols(b, n)].bitcast(FP8X4),
+                scales=ys[4 * (b // 2) : P, cols(b % 2, n)],
+                in_=yb[b, n][:],
             )
 
         def store_words(b, n):
@@ -251,11 +253,11 @@ def tile_picked_embpos_none_po_kernel(
         second_layer(5)
         add_block(7)
         second_layer(6)
+        quant_y(2)
         second_layer(7)
         new_yb(7)
         round_scalar(7)
 
-        quant_y(2)
         new_yb(3)
         new_yb(4, 2)
         new_yb(6)
@@ -271,4 +273,5 @@ def tile_picked_embpos_none_po_kernel(
 
         for q in range(4):
             eng = nc.sync if q % 2 == 0 else nc.scalar
-            eng.dma_start(out_2[0, q:16:4, :].bitcast(I32), ys[q:P:32, :].bitcast(I32))
+            rows = out_2[0, 4 * q : 4 * q + 4, :].bitcast(I32).rearrange("r (j c) -> j r c", j=4)
+            eng.dma_start(rows, ys[32 * q : 32 * q + 16, :].bitcast(I32))

@@ -46,7 +46,7 @@ def tile_picked_embpos_none_po_kernel(
             return lay.tile(shape, dtype, name=name, offset=at * QUARTER, align_bytes=64)
 
         w1_at = (0, 16)
-        pos_at = (36, 44, 60, 84)
+        pos_at = (36, 152, 60, 176)
         h_at = {b: pos_at[0] if b == 1 else 100 + 4 * b for b in range(NBLK)}
         words_at = {0: 16, 1: 18, 4: 22, 3: 16}
         yb_at = {0: 132, 2: 140, 3: pos_at[3] + 12, 4: pos_at[3], 6: pos_at[3] + 8, 7: 148}
@@ -60,7 +60,8 @@ def tile_picked_embpos_none_po_kernel(
         w2w_raw = keep.tile([P, 2 * H], U8, name="w2w_raw", align_bytes=64)
         w1_raw = [laid([P, PACK, hi - lo], F32, f"w1_raw{a}", w1_at[a]) for a, (lo, hi) in enumerate(W1_PIECES)]
         pos_sb = [
-            laid([P, PACK, (hi - lo) * BLK], F32, f"pos{c}", pos_at[c]) for c, (lo, hi) in enumerate(POS_CHUNKS)
+            laid([P, PACK, ((hi - lo) | 1) * BLK], F32, f"pos{c}", pos_at[c])[:, :, 0 : (hi - lo) * BLK]
+            for c, (lo, hi) in enumerate(POS_CHUNKS)
         ]
 
         nc.vector.memset(xs[:].bitcast(I32), 0)
@@ -79,7 +80,7 @@ def tile_picked_embpos_none_po_kernel(
 
         def load_pos(c):
             lo, hi = POS_CHUNKS[c]
-            nc.sync.dma_start(pos_sb[c][:], pos_rows[:, :, lo * BLK : hi * BLK])
+            nc.sync.dma_start(pos_sb[c], pos_rows[:, :, lo * BLK : hi * BLK])
 
         load_pos(0)
         for q in range(4):

from contextlib import ExitStack

import concourse.mybir as mybir

K, T, S, H = 512, 2048, 1024, 512
FLOPS = 2 * K * H * S + 2 * H * H * S

F32 = mybir.dt.float32
BF16 = mybir.dt.bfloat16
I32 = mybir.dt.int32
U32 = mybir.dt.uint32
U16 = mybir.dt.uint16
U8 = mybir.dt.uint8
FP8X4 = mybir.dt.float8_e4m3fn_x4
FP4X4 = mybir.dt.float4_e2m1fn_x4

P = 128
PACK = 4
BLK = 128
NBLK = S // BLK
QUARTER = 256
BANK = 2048
RUN = 2
W1_FIRST = 224
W1_PIECES = ((0, W1_FIRST), (W1_FIRST, H))
CAST_POOL = 24
POS_CHUNKS = ((0, 1), (1, 3), (3, 6), (6, 8))


def chunk_of(chunks, b):
    return [n for n, (lo, hi) in enumerate(chunks) if lo <= b < hi][0]


def tile_picked_embpos_none_po_kernel(
    tc, x_words, x_scales, w1, w2_words, w2_scales, pos, offs, out_0, out_1, out_2
):
    nc = tc.nc
    add = mybir.AluOpType.add
    with ExitStack() as ctx:
        keep = ctx.enter_context(tc.tile_pool(name="keep", bufs=1))
        lay = ctx.enter_context(tc.tile_pool(name="lay", bufs=1))
        ps_h = ctx.enter_context(tc.psum_pool(name="ps_h", bufs=1))
        ps_y = ctx.enter_context(tc.psum_pool(name="ps_y", bufs=5))

        def laid(shape, dtype, name, at):
            return lay.tile(shape, dtype, name=name, offset=at * QUARTER, align_bytes=64)

        w1_at = (0, 16)
        pos_at = (36, 152, 60, 176)
        h_at = {b: pos_at[0] if b == 1 else 100 + 4 * b for b in range(NBLK)}
        words_at = {0: 16, 1: 18, 4: 22, 3: 16}
        yb_at = {0: 132, 2: 140, 3: pos_at[3] + 12, 4: pos_at[3], 6: pos_at[3] + 8, 7: 148}
        yc_at = pos_at[2]
        bank_of = {b: b % 3 for b in range(NBLK)}

        offsets = keep.tile([P, S // 16], U16, name="offsets")
        xw = keep.tile([P, T], I32, name="xw", align_bytes=64)
        xs = keep.tile([P, T], U8, name="xs", align_bytes=64)
        w2s_raw = keep.tile([P, H], U8, name="w2s_raw", align_bytes=64)
        w2w_raw = keep.tile([P, 2 * H], U8, name="w2w_raw", align_bytes=64)
        w1_raw = [laid([P, PACK, hi - lo], F32, f"w1_raw{a}", w1_at[a]) for a, (lo, hi) in enumerate(W1_PIECES)]
        pos_sb = [
            laid([P, PACK, ((hi - lo) | 1) * BLK], F32, f"pos{c}", pos_at[c])[:, :, 0 : (hi - lo) * BLK]
            for c, (lo, hi) in enumerate(POS_CHUNKS)
        ]

        nc.vector.memset(xs[:].bitcast(I32), 0)
        nc.vector.memset(w2s_raw[:].bitcast(I32), 0)

        x_rows = x_words[0].rearrange("p n t -> p (n t)").bitcast(I32)
        w1_rows = w1.rearrange("(p j) c -> p j c", j=PACK)
        pos_rows = pos.rearrange("(p t) n -> p t n", t=PACK)
        nc.sync.dma_start(w1_raw[0][:], w1_rows[:, :, 0:W1_FIRST])
        nc.sync.dma_start(offsets[:], offs)
        for q in range(4):
            eng = nc.sync if q % 2 == 0 else nc.scalar
            eng.dma_start(xs[q:P:32, :].bitcast(I32), x_scales[0, q:16:4, :].bitcast(I32))
        nc.sync.dma_start(w1_raw[1][:], w1_rows[:, :, W1_FIRST:H])
        nc.sync.dma_start(xw[:], x_rows)

        def load_pos(c):
            lo, hi = POS_CHUNKS[c]
            nc.sync.dma_start(pos_sb[c], pos_rows[:, :, lo * BLK : hi * BLK])

        load_pos(0)
        for q in range(4):
            nc.sync.dma_start(w2s_raw[q:P:32, :].bitcast(I32), w2_scales[0, q:16:4, :].bitcast(I32))
        nc.sync.dma_start(w2w_raw[:].bitcast(I32), w2_words[0].bitcast(I32))
        for c in range(1, len(POS_CHUNKS)):
            load_pos(c)

        gs = keep.tile([P, S], U8, name="gs", align_bytes=64)
        nc.vector.tensor_copy(gs[:], xs[:].indirect(offsets[:]))

        w1b = keep.tile([P, PACK * H], BF16, name="w1b", align_bytes=64)
        w1c = keep.tile([P, H], U32, name="w1c", align_bytes=64)
        w1s = keep.tile([P, H], U8, name="w1s", align_bytes=64)
        w1b_v = w1b[:].rearrange("p (t m j) -> p m t j", t=PACK, j=PACK)
        w1_v = [raw[:].rearrange("p j (m t) -> p m t j", t=PACK) for raw in w1_raw]
        m_first, m_cut = W1_FIRST // PACK, P - CAST_POOL
        nc.scalar.copy(w1b_v[:, 0:m_first], w1_v[0])
        nc.scalar.copy(w1b_v[:, m_first:m_cut], w1_v[1][:, 0 : m_cut - m_first])
        nc.gpsimd.tensor_copy(w1b_v[:, m_cut:P], w1_v[1][:, m_cut - m_first : P - m_first])
        nc.vector.quantize_mx(out=w1c[:].bitcast(FP8X4), scales=w1s[:], in_=w1b[:])

        w2w = keep.tile([P, 2 * H], U8, name="w2w", align_bytes=64)
        nc.scalar.copy(
            w2w[:].bitcast(U16).rearrange("p (t m) -> p t m", t=PACK),
            w2w_raw[:].bitcast(U16).rearrange("p (m t) -> p t m", t=PACK),
        )
        w2s = keep.tile([P, H], U8, name="w2s", align_bytes=64)
        nc.gpsimd.tensor_copy(
            w2s[:].rearrange("p (t m) -> p t m", t=PACK),
            w2s_raw[:].rearrange("p (m t) -> p t m", t=PACK),
        )

        ys = keep.tile([P, 2 * BLK], U8, name="ys", align_bytes=64)
        out_rows = out_0.rearrange("(p t) n -> p t n", t=PACK)
        out_words = out_1[0].rearrange("p n t -> p (n t)").bitcast(I32)
        gw, acc_h, hb, hq, acc_y, y_sb, yb, late = {}, {}, {}, {}, {}, {}, {}, {}

        def cols(b, n=1):
            return slice(b * BLK, (b + n) * BLK)

        def gather_words(b, n=1):
            g = laid([P, n * BLK], U32, f"gw{b}", words_at[b])
            per = BLK // 16
            nc.vector.tensor_copy(g[:], xw[:].bitcast(U32).indirect(offsets[:, per * b : per * (b + n)]))
            for i in range(n):
                gw[b + i] = g[:, cols(i)]

        def first_product(b):
            acc = ps_h.tile([P, PACK, BLK], F32, name=f"acc_h{b}", offset=bank_of[b] * BANK)
            for t in range(PACK):
                nc.tensor.matmul_mx(
                    out=acc[:, t, :],
                    lhsT=w1c[:, t * P : (t + 1) * P].bitcast(FP8X4),
                    lhsT_scale=w1s[:, t * P : (t + 1) * P],
                    rhs=gw[b].bitcast(FP8X4),
                    rhs_scale=gs[:, cols(b)],
                    start=True,
                    stop=True,
                )
            acc_h[b] = acc

        def pos_block(b):
            c = chunk_of(POS_CHUNKS, b)
            return pos_sb[c][:, :, cols(b - POS_CHUNKS[c][0])]

        def new_h(b, n=1):
            tile = laid([P, n * PACK * BLK], BF16, f"h{b}", h_at[b])
            for i in range(n):
                hb[b + i] = tile[:, i * PACK * BLK : (i + 1) * PACK * BLK]
            hb[b, n] = tile

        def add_pos(b):
            nc.vector.tensor_tensor(
                hb[b].rearrange("p (c i t) -> p c t i", i=RUN, t=PACK),
                acc_h[b][:].rearrange("p t (c i) -> p c t i", i=RUN),
                pos_block(b).rearrange("p t (c i) -> p c t i", i=RUN),
                add,
            )

        def quant_h(b, n=1):
            hc = keep.tile([P, n * BLK], U32, name=f"hc{b}", align_bytes=64)
            hs = keep.tile([P, n * BLK], U8, name=f"hs{b}", align_bytes=64)
            nc.vector.quantize_mx(out=hc[:].bitcast(FP8X4), scales=hs[:], in_=hb[b, n][:])
            for i in range(n):
                hq[b + i] = hc[:, cols(i)], hs[:, cols(i)]

        def second_product(b):
            hc, hs = hq[b]
            acc = ps_y.tile([P, PACK, BLK], F32, name="acc_y")
            for t in range(PACK):
                nc.tensor.matmul_mx(
                    out=acc[:, t, :],
                    lhsT=w2w[:, 2 * t * P : 2 * (t + 1) * P].bitcast(FP4X4),
                    lhsT_scale=w2s[:, t * P : (t + 1) * P],
                    rhs=hc.bitcast(FP8X4),
                    rhs_scale=hs,
                    start=True,
                    stop=True,
                )
            acc_y[b] = acc

        def leave(b):
            y_sb[b] = keep.tile([P, PACK, BLK], F32, name=f"y{b}", align_bytes=64)
            nc.scalar.copy(y_sb[b][:], acc_y[b][:])
            nc.sync.dma_start(out_rows[:, :, cols(b)], y_sb[b][:])

        def new_yb(b, n=1):
            tile = laid([P, n * PACK * BLK], BF16, f"yb{b}", yb_at[b])
            for i in range(n):
                yb[b + i] = tile[:, i * PACK * BLK : (i + 1) * PACK * BLK]
            yb[b, n] = tile

        def round_scalar(b):
            nc.scalar.copy(yb[b].rearrange("p (n t) -> p n t", t=PACK), acc_y[b][:].rearrange("p t n -> p n t"))

        def round_vector(b):
            nc.vector.tensor_copy(
                yb[b].rearrange("p (c i t) -> p c t i", i=RUN, t=PACK),
                y_sb[b][:].rearrange("p t (c i) -> p c t i", i=RUN),
            )

        def quant_y(b, n=1):
            nc.vector.quantize_mx(
                out=late["yc"][:, cols(b, n)].bitcast(FP8X4),
                scales=ys[4 * (b // 2) : P, cols(b % 2, n)],
                in_=yb[b, n][:],
            )

        def store_words(b, n):
            nc.sync.dma_start(out_words[:, cols(b, n)], late["yc"][:, cols(b, n)])

        def add_block(b):
            new_h(b)
            add_pos(b)

        def second_layer(b):
            quant_h(b)
            second_product(b)
            leave(b)

        gather_words(0)
        first_product(0)
        gather_words(1, 2)
        first_product(1)
        first_product(2)
        gather_words(4, 4)
        new_yb(0, 2)
        new_yb(2)
        add_block(0)
        gather_words(3)
        quant_h(0)
        second_product(0)
        first_product(3)
        leave(0)
        round_scalar(0)
        add_block(1)
        first_product(4)
        for b in (2, 3, 4):
            add_block(b)
            first_product(b + 3)
            second_layer(b - 1)
            if b < 4:
                round_scalar(b - 1)
        add_block(5)
        second_layer(4)
        late["yc"] = laid([P, S], I32, "yc", yc_at)
        quant_y(0, 2)
        store_words(0, 2)
        add_block(6)
        second_layer(5)
        add_block(7)
        second_layer(6)
        quant_y(2)
        second_layer(7)
        new_yb(7)
        round_scalar(7)

        new_yb(3)
        new_yb(4, 2)
        new_yb(6)
        for b in (3, 4, 5):
            round_vector(b)
        quant_y(3)
        round_vector(6)
        quant_y(4, 2)
        store_words(2, 4)
        quant_y(6)
        quant_y(7)
        store_words(6, 2)

        for q in range(4):
            eng = nc.sync if q % 2 == 0 else nc.scalar
            rows = out_2[0, 4 * q : 4 * q + 4, :].bitcast(I32).rearrange("r (j c) -> j r c", j=4)
            eng.dma_start(rows, ys[32 * q : 32 * q + 16, :].bitcast(I32))
